import numpy as np, ml_dtypes
CORES = [3,11,19,27,35,43,51,59]
N = 8
import mx_ref
BF = ml_dtypes.bfloat16
def gentries(a):
    return np.ascontiguousarray(a.reshape(8, 16, -1).transpose(0, 2, 1)).reshape(8, -1)
def gtable(e):
    e = np.asarray(e); return np.ascontiguousarray(e.reshape(8, -1, 16).transpose(0, 2, 1)).reshape(128, -1).astype(np.int32)
def gcols(t, e):
    v = np.concatenate([t.reshape(8, 16, -1, 4), np.zeros((8, 16, 1, 4), BF)], axis=2)
    return np.ascontiguousarray(np.stack([v[g][:, e[g]] for g in range(8)])).reshape(128, -1)
def gpick(z, e):
    return np.concatenate([z[16 * g:16 * g + 16][:, e[g]] for g in range(8)])
def tile(rs):
    return np.stack(rs, axis=2).reshape(128, -1).astype(BF)
def pick(q, e):
    c = np.concatenate([q[0].reshape(128, -1, 4), np.zeros((128, 1, 4), np.uint8)], axis=1); s = np.concatenate([q[1], np.ones((16, 1), np.uint8)], axis=1)
    return (np.ascontiguousarray(c[:, e].reshape(128, -1)), np.ascontiguousarray(s[:, e]))
def join(*qs):
    return (np.concatenate([q[0] for q in qs], axis=1), np.concatenate([q[1] for q in qs], axis=1))
def put(q, e, v):
    c, s = q[0].reshape(128, -1, 4).copy(), q[1].copy(); c[:, e] = v[0].reshape(128, -1, 4); s[:, e] = v[1]
    return (c.reshape(128, -1), s)
def pk(c, s):
    return (np.ascontiguousarray(c), mx_ref.live(s))
def emit(q):
    return q[0], q[1]
def packed(v, rng):
    q = [mx_ref.quantize(np.ascontiguousarray(v[r])) for r in range(N)]
    return np.stack([a for a, b in q]), np.stack([mx_ref.plane(b, rng) for a, b in q])
def values_of_codes():
    e, c = np.zeros((128, 128, 4), np.float32), np.zeros((128, 2, 4), np.uint8)
    e[np.arange(128), np.arange(128), 0] = 1
    c[:127, :, 0] = np.arange(256).reshape(2, 128).T[:127]
    return mx_ref.matmul(mx_ref.quantize(e.reshape(128, 512).astype(BF)), (c.reshape(128, 8), np.full((16, 2), 127, np.uint8))).T.reshape(-1).astype(np.float64)
CODE_VALUE, SCALE_VALUE = values_of_codes(), 2.0 ** (np.arange(256) - 127.0)
def decode(q):
    return (CODE_VALUE[q[0]].reshape(16, 8, -1, 4) * SCALE_VALUE[q[1]][:, None, :, None] + 0.0).reshape(128, -1).astype(np.float32)
def f(rng, *shape):
    return mx_ref.flush((rng.standard_normal(shape, dtype=np.float32) * np.exp2(rng.integers(-2, 3, shape[:-1] + (1,)))).astype(BF))
def wide(rng, *shape, cols=0):
    v = rng.standard_normal(shape, dtype=np.float32) * np.exp2(rng.integers(-12, 13, shape)).astype(np.float32)
    if cols: v *= np.repeat(np.exp2(rng.integers(-cols, cols + 1, shape[:-2] + (1, shape[-1] // 4))) * (rng.random(shape[:-2] + (1, shape[-1] // 4)) > 0.0625), 4, axis=-1).astype(np.float32)
    return mx_ref.flush(v.astype(BF))
C = 352
STEP = [1, 2, 4]
def numbers_of(rng):
    return {"x": np.array(f(rng, N, 128, 4 * C)), "u": np.array(f(rng, N, 128, 512)), "v": np.array(f(rng, N, 128, 512))}
def stored(k):
    return {"od": np.stack([gtable(k[r]) for r in range(N)])}
def orders(rng):
    return stored(rng.permuted(np.tile(np.arange(C), (N, 8, 1)), axis=2))
def rings(rng):
    h = rng.permutation(8)
    pairs = [1] + [2] * (C // 2 - 1) + [1]
    sizes = [[C], [C], [1, C - 1], [257, C - 257], pairs, pairs, [C // 2, C // 2], [1] * C]
    i = np.arange(N)
    odd = (i ^ (i >> 1) ^ (i >> 2)) % 2
    k = np.zeros((N, 8, C), np.int64)
    for g in range(8):
        w = np.arange(C) if h[g] % 2 == 0 else rng.permutation(C)
        c, after = rng.permutation(C), np.zeros(C, np.int64)
        a = 0
        for m in sizes[h[g]]:
            after[w[a:a + m]] = np.roll(w[a:a + m], -1)
            a += m
        k[:, g] = np.where(odd[:, None] == 1, c[after], c)
    return stored(k)
def layers(rng):
    return np.array(f(rng, N, 128, 2048)).reshape(N, 8, 16, 4, 8, 16, 4)
def weights(rng, w):
    c, s = packed(np.ascontiguousarray(w).reshape(N, 128, 2048), rng)
    return {"wc": c, "ws": s}
def setup_inputs(rng):
    return {**numbers_of(rng), **orders(rng), **weights(rng, layers(rng))}
def setup_inputs_ties(rng):
    d = numbers_of(rng)
    o = rng.permutation(N)
    k = rng.integers(-1, 2, (N, 8, C)).astype(np.float32)
    k[o[0]] = 0
    k[o[1]] = 1
    k[o[2]] = -1
    x = d["x"].reshape(N, 8, 16, C, 4)
    x[:, :, 0] = 0
    x[:, :, 0, :, 0] = k.astype(BF)
    u = d["u"].reshape(N, 128, 128, 4)
    u[:, :, ::16] = 0
    for h in range(0, 128, 16): u[:, h, h, 0] = 1
    w = layers(rng)
    w[:, :, :, :, :, 0] = 0
    return {"x": x.reshape(N, 128, 4 * C), "u": u.reshape(N, 128, 512), "v": d["v"], **rings(rng), **weights(rng, w)}
def setup_inputs_near(rng):
    d = numbers_of(rng)
    small = ((np.arange(N) & STEP[1]) > 0) ^ (rng.random() < 0.5)
    k = np.where(small, 2.0 ** -30, 1.0)
    x = d["x"].astype(np.float32).reshape(N, 8, 16, C, 4)
    x[:, :, :8] = 0
    s = rng.integers(-1, 2, (N, 8, C)) * k[:, None, None]
    x[:, :, 0, :, 0] = 1.125 * s
    x[:, :, 1, :, 0] = -1.25 * s
    x[:, :, 2, :, 0] = rng.choice([-1.0, 1.0], (N, 8, C)) * 2.0 ** -30
    x[:, :, 4, :, 0] = 2.0 ** -30
    for r in range(N):
        at = [0, C - 1, int(rng.integers(C)), int(rng.integers(C))]
        for g, j in zip(rng.permutation(8)[:4], at): x[r, g, 0, j, 0] = 2.0 ** 30 * rng.choice([-1.0, 1.0])
    k = k.astype(np.float32)
    u = d["u"].reshape(N, 128, 128, 4)
    u[:, :, ::16] = 0
    for h in range(0, 128, 16):
        u[:, h, h, 0] = (1.125 * k).astype(BF)
        u[:, h + 1, h, 0] = k.astype(BF)
        u[:, h + 3, h, 0] = k.astype(BF)
    w = layers(rng)
    w[:, :, :8] = 0
    w[:, :, :, :, :, :8] = 0
    for r in range(N):
        for g in range(8):
            if small[r]: w[r, g, 2, 0, g, 3, 0] = 2.0 ** -8
    return {"x": x.reshape(N, 128, 4 * C).astype(BF), "u": u.reshape(N, 128, 512), "v": d["v"], **orders(rng), **weights(rng, w)}
def setup_inputs_odd(rng):
    d = numbers_of(rng)
    x = (1.0 + (2 * rng.integers(0, 64, (N, 16, 8, C, 4)) + 1) * 2.0 ** -7) * np.exp2(-rng.integers(0, 7, (N, 16, 8, C, 4)).astype(np.float64)) * rng.choice([-1.0, 1.0], (N, 16, 8, C, 4))
    x[:, :, 0, :, 0] = np.where(rng.random((N, 16, C)) < 0.5, 1.96875, 1.875) * 2.0 ** 8 * rng.choice([-1.0, 1.0], (N, 16, 1))
    x[:, ::2, 1, :, 0] = rng.integers(7, 10, (N, 8, C)) * 2.0 ** -8
    x[:, ::2, 2, :, 0] = -8 * 2.0 ** -8
    u = d["u"].reshape(N, 16, 8, 128, 4)
    u[:, :, :, ::16] = 0
    for g in range(8): u[:, 2 * g, 1:3, 16 * g, 0] = 1
    w = layers(rng)
    for i in (0, 8):
        w[:, :, i] = 0
        w[:, :, :, :, :, i] = 0
    return {"x": x.astype(np.float32).reshape(N, 128, 4 * C).astype(BF), "u": u.reshape(N, 128, 512), "v": d["v"], **orders(rng), **weights(rng, w)}
def setup_inputs_ends(rng):
    d = numbers_of(rng)
    o, most = rng.permutation(N) % 4, rng.permutation(N) % 2
    h, e = rng.permutation(8), int(rng.integers(8))
    c = np.where(h < 2, 0.0, h % 2 * 2.0 - 1.0)[None, :, None]
    k = np.array([2.0, 4.0])[rng.permutation(8) % 2]
    x = np.zeros((N, 8, 16, C, 4))
    u = d["u"].astype(np.float32).reshape(N, 128, 128, 4)
    v = np.zeros((N, 128, 512), np.float32)
    w = np.zeros((N, 128, 4, 128, 4), np.float32)
    i = np.arange(128)
    for r in range(N):
        low = -0.7 * (0.9 + 0.1 * rng.random((8, 16, C, 4))) * 2.0 ** 30
        tiny = -(1.0 + 0.125 * rng.integers(0, 8, (8, 16, C, 4))) * 2.0 ** -30
        if o[r] == 0: x[r] = low
        if o[r] == 1: x[r] = np.where((rng.random(C) < 0.5)[:, None], 0.7 * (1.0 + 0.4 * rng.random((8, 16, C, 4))) * 2.0 ** 27, low)
        if o[r] == 2: x[r] = tiny
        if o[r] == 3: x[r] = d["x"][r].astype(np.float32).reshape(8, 16, C, 4)[:, :, :1]
        x[r, e, 8:] = tiny[e, 8:, :1] if o[r] == 3 else tiny[e, 8:]
        if o[r] < 2: u[r, :, ::16] = c * (0.9 + 0.1 * rng.random((128, 8, 4))) * 2.0 ** 30
        if o[r] == 2: u[r, :, ::16] = c * (1.0 + 0.125 * rng.integers(0, 8, (128, 8, 4))) * 2.0 ** -30
        if o[r] == 3: u[r, :, ::16] *= np.abs(c).astype(np.float32)
        a = (0.9 + 0.1 * rng.random((128, 512))) * 2.0 ** 30 if o[r] < 2 else (1.0 + 0.125 * rng.integers(0, 8, (128, 512))) * 2.0 ** -30
        v[r] = rng.choice([-1.0, 1.0], (128, 512)) * a
        t = k[i // 16]
        t[16 * e + 8:16 * e + 16] = 2.0 ** 8 if most[r] else 2.0 ** -8
        for b in range(4): w[r, i, b, i, b] = t
    return {"x": x.astype(np.float32).reshape(N, 128, 4 * C).astype(BF), "u": u.reshape(N, 128, 512).astype(BF), "v": v.astype(BF), **rings(rng), **weights(rng, w.astype(BF))}
def setup_inputs_spread(rng):
    d = setup_inputs(rng)
    d["x"] = wide(rng, N, 128, 4 * C, cols=6)
    return d
def check_inputs(d):
    b = []
    for k in ("x", "u", "v"):
        a = np.abs(d[k].astype(np.float32))
        if not (np.isfinite(a).all() and ((a == 0) | (a >= 2.0 ** -30) & (a <= 2.0 ** 30)).all()): b.append("a value of " + k)
    none, least, most = [emit(mx_ref.quantize(np.full((128, 16), k, np.float32).astype(BF)))[1][0, 0] for k in (0.0, 2.0 ** -8, 2.0 ** 8)]
    for r in range(N):
        if not (np.sort(gentries(d["od"][r]), axis=1) == np.arange(C)).all(): b.append("od: a group whose entries are not all columns once")
        if ((d["wc"][r] == 0x7F) | (d["wc"][r] == 0xFF)).any(): b.append("wc: a code that is no number")
        s = mx_ref.live(d["ws"][r])
        if ((s != none) & ((s < least) | (s > most))).any(): b.append("ws: a scale out of range")
        if (((d["wc"][r].reshape(16, 8, 512, 4) & 0x7F) != 0) & (s == none)[:, None, :, None]).any(): b.append("wc: a code other than zero under the scale of zeros")
    return b
def at(t, e):
    return np.take_along_axis(t, e, axis=1)
def reference(x, u, v, od, wc, ws):
    qu = [mx_ref.quantize(u[r]) for r in range(N)]
    lay = [pk(wc[r], ws[r]) for r in range(N)]
    now = [x[r] for r in range(N)]
    order = [gentries(od[r]).astype(np.int64) for r in range(N)]
    for step in STEP:
        old, order, far, z = order, [], [], []
        for r in range(N):
            q = mx_ref.quantize(now[r])
            s = mx_ref.matmul(qu[r], q)[::16]
            mine, other = old[r], old[r ^ step]
            jump = at(np.argsort(other, axis=1), mine)
            low = np.tile(np.arange(C), (8, 1))
            for i in range(9):
                low = np.minimum(low, at(low, jump))
                jump = at(jump, jump)
            order.append(np.where(at(s, at(mine, low)) > 0, other, mine))
            far.append(decode(q))
            t = far[r].astype(BF)
            pair = gcols(t, order[r]).astype(np.float32) + gcols(t, at(order[r], order[r])).astype(np.float32)
            z.append(mx_ref.quantize((pair * np.float32(0.5)).astype(BF)))
        for r in range(N):
            back = np.argsort(order[r], axis=1)
            now[r] = tile([gpick(mx_ref.matmul(pick(lay[r], np.arange(128 * b, 128 * b + 128)), z[r ^ step]) * np.float32(0.03125), back) + far[r][:, b::4] for b in range(4)])
    y, fo = np.zeros((N, 128, C), np.float32), np.zeros((N, 8, C), np.float32)
    oc, osc = np.zeros((N, 128, 4 * C), np.uint8), np.zeros((N, 16, C), np.uint8)
    for r in range(N):
        q = mx_ref.quantize(now[r])
        y[r] = mx_ref.matmul(mx_ref.quantize(v[r]), q)
        fo[r] = order[r]
        oc[r], osc[r] = emit(q)
    return {"y": y, "fo": fo, "oc": oc, "osc": osc}

@@ -1,0 +1,303 @@
+from concourse.bass import DstId, RemoteDMATransfer
+from concourse.mybir import dt, AluOpType, ActivationFunctionType
+
+C, K = 352, 22
+HALF = 176
+BIG = 2.0 ** 30
+STEP = [1, 2, 4]
+NJ = 8
+CFG = {"pre": 2, "jfirst": True, "gap": [2, 3, 4], "dup": "-bvvvvvv"}
+KEEP = 3
+
+SCRATCH = {
+    "odl": ("sbuf", [128, K], "int32"), "pc": ("sbuf", [128, C], "bfloat16"),
+    "dd": ("sbuf", [128, C], "int32"), "dm": ("sbuf", [128, C], "int32"),
+    "ma": ("sbuf", [128, C], "float32"), "mb": ("sbuf", [128, C], "float32"),
+    "mk": ("sbuf", [128, C], "bfloat16"), "sc": ("sbuf", [128, 1], "float32"),
+    "ones": ("sbuf", [128, 128], "bfloat16"), "idn": ("sbuf", [128, 128], "bfloat16"),
+    "et": ("sbuf", [128, 2048], "bfloat16"),
+    "eq": ("sbuf", [128, 512], "float8_e4m3fn_x4"), "es": ("sbuf", [128, 512], "uint8"),
+    "ut": ("sbuf", [128, 512], "bfloat16"), "vt": ("sbuf", [128, 512], "bfloat16"),
+    "uq": ("sbuf", [128, 128], "float8_e4m3fn_x4"), "us": ("sbuf", [128, 128], "uint8"),
+    "u2q": ("sbuf", [128, 128], "float8_e4m3fn_x4"), "u2s": ("sbuf", [128, 128], "uint8"),
+    "ul": ("sbuf", [128, 8], "int32"), "uo": ("sbuf", [128, 8], "uint16"),
+    "vq": ("sbuf", [128, 128], "float8_e4m3fn_x4"), "vs": ("sbuf", [128, 128], "uint8"),
+    "wq": ("sbuf", [128, 512], "float8_e4m3fn_x4"), "wp": ("sbuf", [128, 512], "uint8"),
+    "ps": ("psum", [128, 4096], "float32"),
+    "ya": ("sbuf", [128, C], "float32"), "fr": ("sbuf", [128, C], "float32"),
+}
+for _r in range(4):
+    SCRATCH["x%d" % _r] = ("sbuf", [128, 4 * C], "bfloat16")
+    SCRATCH["xq%d" % _r] = ("sbuf", [128, C], "float8_e4m3fn_x4")
+    SCRATCH["xs%d" % _r] = ("sbuf", [128, C], "uint8")
+    SCRATCH["o%d" % _r] = ("sbuf", [128, K], "uint16")
+    SCRATCH["inv%d" % _r] = ("sbuf", [128, C], "bfloat16")
+for _r in range(3):
+    SCRATCH["oin%d" % _r] = ("sbuf", [128, K], "uint16")
+    SCRATCH["f%d" % _r] = ("sbuf", [128, 4 * C], "bfloat16")
+    SCRATCH["a%d" % _r] = ("sbuf", [128, 4 * C], "float32")
+    SCRATCH["z%d" % _r] = ("sbuf", [128, 4 * C], "bfloat16")
+    SCRATCH["rb%d" % _r] = ("sbuf", [128, 4 * C], "float32")
+    SCRATCH["hs%d" % _r] = ("sbuf", [128, C], "float32")
+    SCRATCH["zq%d" % _r] = ("sbuf", [128, C], "float8_e4m3fn_x4")
+    SCRATCH["zs%d" % _r] = ("sbuf", [128, C], "uint8")
+    SCRATCH["xi%d" % _r] = ("sbuf", [128, C], "float8_e4m3fn_x4")
+    SCRATCH["xp%d" % _r] = ("sbuf", [128, C], "uint8")
+    SCRATCH["fd%d" % _r] = ("sbuf", [128, 4 * C], "bfloat16")
+    SCRATCH["oz%d" % _r] = ("sbuf", [128, K], "uint16")
+    SCRATCH["jr%d" % _r] = ("sbuf", [128, NJ * C], "bfloat16")
+    SCRATCH["lr%d" % _r] = ("sbuf", [128, 9 * C], "bfloat16")
+    SCRATCH["le%d" % _r] = ("sbuf", [128, NJ * C], "bfloat16")
+    SCRATCH["fe%d" % _r] = ("sbuf", [128, 4 * C], "bfloat16")
+    SCRATCH["sr%d" % _r] = ("sbuf", [128, 11 * C], "bfloat16")
+    SCRATCH["tb%d" % _r] = ("sbuf", [128, 10 * K], "uint16")
+    SCRATCH["sg%d" % _r] = ("sbuf", [128, 3 * C], "bfloat16")
+    SCRATCH["sm%d" % _r] = ("sbuf", [128, 8 * K], "float32")
+SEMAPHORES = (["sv", "ss", "st", "sg", "loc", "sto"] + ["l" + n for n in ("od", "x", "u", "v", "w", "p")]
+              + [n + str(r) for n in ("ro", "rx", "rl") for r in range(3)])
+
+
+def rank_program(g, core, T, topo):
+    rank = T.rank_of(core)
+    if rank is None:
+        return
+    A, F = AluOpType, ActivationFunctionType
+    Q = {"v": g.vector, "s": g.scalar, "t": g.tensor, "g": g, "y": g.sync}
+    own = {"v": "sv", "s": "ss", "t": "st", "g": "sg"}
+    done, seen = {}, {}
+
+    def wait(q, after):
+        need = {}
+        for h in after:
+            if h is not None:
+                need[h[0]] = max(need.get(h[0], 0), h[1])
+        for name, n in need.items():
+            if seen.get((q, name), 0) < n:
+                Q[q].wait_ge(T.sem[name], n)
+                seen[(q, name)] = n
+
+    def do(q, after, call, *args, **kw):
+        wait(q, after)
+        s = own[q]
+        call(*args, **kw).then_inc(T.sem[s], 1)
+        done[s] = done.get(s, 0) + 1
+        return (s, done[s])
+
+    def dma(q, after, s, out, in_):
+        wait(q, after)
+        Q[q].dma_start(out, in_).then_inc(T.sem[s], 16)
+        done[s] = done.get(s, 0) + 16
+        return (s, done[s])
+
+    def send(after, dst, s, out, in_):
+        wait("g", after)
+        rid, pid = topo.addr(dst)[:2]
+        g.remote_dma(out, in_, T.sem[s], T.sem["loc"], pid, rid, topo.mask(core, dst))
+        done["loc"] = done.get("loc", 0) + len(topo.engines(core, dst))
+
+    def send_list(after, src, parts):
+        wait("g", after)
+        n = len(topo.engines(core, parts[0][0])) // len(parts)
+        tr = []
+        for i, (dst, s, out) in enumerate(parts):
+            rid, pid = topo.addr(dst)[:2]
+            m = sum(1 << e for e in topo.engines(core, dst)[n * i:n * i + n])
+            tr.append(RemoteDMATransfer(dst_ids=[DstId(rid=rid, pnc=pid)], dma_engine_mask=m, remote_sem=T.sem[s], src=src, dst=out))
+        g.remote_dma_fused(tr, local_sem=T.sem["loc"])
+        done["loc"] = done.get("loc", 0) + n * len(parts)
+
+    V, S, PE = g.vector, g.scalar, g.tensor
+
+    def blk(t, b, n=C):
+        return t[:, b * n:(b + 1) * n]
+
+    def bank(k, n=C):
+        return T.ps[:, 512 * k:512 * k + n]
+
+    partner = [T.cores[rank ^ s] for s in STEP]
+    h_od = dma("y", [], "lod", T.odl[:], T.od[:, :])
+    h_x = dma("s", [], "lx", T.x0[:], T.x[:, :])
+    h_u = dma("y", [], "lu", T.ut[:], T.u[:, :])
+    h_w = dma("y", [], "lw", T.wq[:].bitcast(dt.uint8), T.wc[:, :])
+    h_p = dma("y", [], "lp", T.wp[:], T.ws[:, :])
+    h_v = dma("s", [], "lv", T.vt[:], T.v[:, :])
+    h_pc = do("g", [], g.iota, T.pc[:], [[1, C]], -HALF, 0, allow_small_or_imprecise_dtypes=True)
+    h_dd = do("g", [], g.iota, T.dd[:], [[1, C]], 128, -1)
+    h_ul = do("g", [], g.iota, T.ul[:], [[16, 8]], 0, 0)
+    h_one = do("v", [], V.memset, T.ones[:], 1.0)
+    h_e0 = do("v", [], V.memset, T.et[:], 0.0)
+    h_o = do("v", [h_od], V.tensor_copy, T.o0[:], T.odl[:])
+    send([h_o], partner[0], "ro0", T.oin0[:], T.o0[:])
+    h_id = do("g", [h_one], g.affine_select, T.idn[:], T.ones[:], [[-1, 128]], A.is_equal, 0.0, 0, 1)
+
+    def scatter(r, h_o):
+        return do("v", [h_o, h_pc], V.tensor_copy, T["inv%d" % r][:].indirect(T["o%d" % r][:]), T.pc[:])
+
+    h_inv = scatter(0, h_o)
+    h_dm = do("v", [h_dd], V.tensor_scalar, T.dm[:], T.dd[:], 15, None, A.bitwise_and)
+    h_sc = do("v", [h_dm], V.tensor_scalar, T.sc[:], T.dm[:, 0:1], 1, 1.0 / BIG, A.is_equal, A.max)
+    h_ma = do("v", [h_dm], V.tensor_scalar, T.ma[:], T.dm[:], 1, BIG, A.is_equal, A.mult)
+    h_mb = do("v", [h_dm], V.tensor_scalar, T.mb[:], T.dm[:], 2, None, A.is_ge)
+    h_mk = do("v", [h_ma, h_mb], V.tensor_tensor, T.mk[:], T.ma[:], T.mb[:], A.add)
+    h_et = [do("v", [h_e0, h_id], V.tensor_copy, T.et[:, 512 * b + b:512 * (b + 1):4], T.idn[:]) for b in range(4)]
+    h_uo = do("v", [h_ul], V.tensor_copy, T.uo[:], T.ul[:])
+    h_uq = do("v", [h_u], V.quantize_mx, T.uq[:], T.us[:], T.ut[:])
+    h_eq = do("v", h_et, V.quantize_mx, T.eq[:], T.es[:], T.et[:])
+    h_u2 = do("v", [h_uq, h_uo], V.tensor_copy, T.u2q[:].bitcast(dt.uint32),
+              T.uq[:].bitcast(dt.uint32).indirect(T.uo[:]))
+    h_u3 = do("v", [h_uq, h_uo], V.tensor_copy, T.u2s[:], T.us[:].indirect(T.uo[:]))
+    h_vq = []
+
+    def quant_x(r, after):
+        return do("v", after, V.quantize_mx, T["xq%d" % r][:], T["xs%d" % r][:], T["x%d" % r][:])
+
+    def mm(k, a, ap, ca, b, bp, after, lo=0, hi=C):
+        return do("t", after, PE.matmul_mx, bank(k, hi - lo), a[:, ca:ca + 128], ap[:, ca:ca + 128],
+                  b[:, lo:hi], bp[:, lo:hi], True, True)
+
+    def table(r, k, row, after):
+        sr = blk(T["sr%d" % r], k)
+        h = do("v", after + [h_mk], V.tensor_tensor_scan, sr, T.mk[:], row, 0.0, A.mult, A.add)
+        return do("v", [h, h_sc], V.tensor_scalar, blk(T["tb%d" % r], k, K),
+                  T["sr%d" % r][:, k * C + 15:(k + 1) * C:16], T.sc[:], HALF + 0.25, A.mult, A.add)
+
+    def products(r, h_q):
+        q, p = T["xq%d" % r], T["xs%d" % r]
+        hs = mm(0, T.u2q, T.u2s, 0, q, p, [h_q, h_u2, h_u3])
+        return [hs] + [mm(1 + b, T.eq, T.es, 128 * b, q, p, [h_q, h_eq]) for b in range(4)]
+
+    def cycles(r, h_inv, h_o):
+        tb, jr, lr, l2, inv, oin = (T[n + str(r)] for n in ("tb", "jr", "lr", "le", "inv", "oin"))
+        arr = ("ro%d" % r, len(topo.engines(partner[r], core)) // (1 if r == 0 else 2))
+        st = {}
+
+        def first():
+            st["j"] = do("s", [arr, h_inv], S.activation, blk(jr, 0), inv[:].indirect(oin[:]), F.Copy)
+            st["l"] = do("v", [arr, h_inv, h_pc], V.tensor_tensor, blk(lr, 0), inv[:].indirect(oin[:]), T.pc[:], A.min)
+            st["t"] = table(r, 0, blk(jr, 0), [st["j"]])
+
+        def step(k):
+            def f():
+                hj = do("s", [st["t"], st["j"]], S.activation, blk(jr, k), blk(jr, k - 1).indirect(blk(tb, k - 1, K)), F.Copy)
+                if k == 1:
+                    prep()
+                if CFG["dup"][k] == "s":
+                    h2 = do("s", [st["l"]], S.activation, blk(l2, k), blk(lr, k - 1), F.Copy)
+                if CFG["dup"][k] == "b":
+                    h2 = do("v", [st["l"]], V.tensor_copy, blk(l2, k), blk(lr, k - 1))
+                ht = table(r, k, blk(jr, k), [hj])
+                if CFG["dup"][k] == "v":
+                    h2 = do("v", [st["l"]], V.tensor_copy, blk(l2, k), blk(lr, k - 1))
+                st["l"] = do("v", [ht, st["l"], h2], V.tensor_tensor, blk(lr, k), blk(lr, k - 1).indirect(blk(tb, k, K)), blk(l2, k), A.min)
+                st["j"], st["t"] = hj, ht
+            return f
+
+        def prep():
+            sm, o = T["sm%d" % r], T["o%d" % r]
+            h1 = do("v", [arr, h_sc], V.tensor_scalar, blk(sm, 0, K), oin[:], T.sc[:], None, A.mult)
+            h2 = do("v", [h_o, h_sc], V.tensor_scalar, blk(sm, 1, K), o[:], T.sc[:], None, A.mult)
+            h3 = do("v", [h_o], V.tensor_scalar, blk(sm, 2, K), o[:], 0.25, None, A.add)
+            h4 = do("v", [h1, h2], V.tensor_tensor, blk(sm, 3, K), blk(sm, 0, K), blk(sm, 1, K), A.subtract)
+            st["prep"] = [h3, h4]
+
+        def last():
+            st["l"] = do("v", [st["t"], st["l"]], V.tensor_tensor, blk(lr, 8), blk(lr, 7).indirect(blk(tb, 7, K)), blk(lr, 6), A.min)
+            st["leader"] = table(r, 8, blk(lr, 8), [st["l"]])
+        return st, [first] + [step(k) for k in range(1, NJ)] + [last]
+
+    h_q = quant_x(0, [h_x])
+    st, steps = cycles(0, h_inv, h_o)
+    steps[0]()
+    at = 1
+    for r in range(3):
+        o, on = T["o%d" % r], T["o%d" % (r + 1)]
+        f, fd, fe, sg, a, z, oz = (T[n + str(r)] for n in ("f", "fd", "fe", "sg", "a", "z", "oz"))
+        send([h_q], partner[r], "rx%d" % r, T["xi%d" % r][:].bitcast(dt.uint8), T["xq%d" % r][:].bitcast(dt.uint8))
+        send([h_q], partner[r], "rx%d" % r, T["xp%d" % r][:], T["xs%d" % r][:])
+        h_pr = products(r, h_q)
+        hf = [None] * 4
+        arr = ("rx%d" % r, 2 * len(topo.engines(partner[r], core)))
+
+        def fcopy(q, b):
+            if q == "v":
+                hf[b] = do("v", [h_pr[1 + b]], V.tensor_copy, blk(f, b), bank(1 + b))
+            else:
+                hf[b] = do("s", [h_pr[1 + b]], S.activation, blk(f, b), bank(1 + b), F.Copy)
+        rest = steps[at:]
+        sign = lambda: do("s", [h_pr[0]], S.activation, blk(sg, 0), bank(0), F.Sign)
+        place = lambda h: do("s", [h, h_o], S.activation, blk(sg, 1), blk(sg, 0).indirect(o[:]), F.Relu)
+        gap = CFG["gap"]
+        for i, s in enumerate(rest):
+            if i == len(rest) - 1:
+                hs = place(sign())
+            s()
+            if i in gap:
+                fcopy("s", gap.index(i))
+        hfl = do("s", [hs, st["leader"]], S.activation, blk(sg, 2), blk(sg, 1).indirect(blk(T["tb%d" % r], 8, K)), F.Copy)
+        hd = []
+        for b in range(4):
+            hm = mm((5 + b) % 8, T.eq, T.es, 128 * b, T["xi%d" % r], T["xp%d" % r], [arr, h_eq, hs])
+            hd.append(do("s", [hm], S.activation, blk(fd, b), bank((5 + b) % 8), F.Copy))
+        for b in range(KEEP):
+            if hf[b] is None:
+                fcopy("s", b)
+        sr, sm = T["sr%d" % r], T["sm%d" % r]
+        h = do("v", [hfl, h_mk], V.tensor_tensor_scan, blk(sr, 9), T.mk[:], blk(sg, 2), 0.0, A.mult, A.add)
+        h = do("v", [h] + st["prep"], V.tensor_tensor, blk(sm, 4, K), sr[:, 9 * C + 15:10 * C:16], blk(sm, 3, K), A.mult)
+        h = do("v", [h], V.tensor_tensor, blk(sm, 5, K), blk(sm, 4, K), blk(sm, 2, K), A.add)
+        h_o = do("v", [h], V.tensor_copy, on[:], blk(sm, 5, K))
+        parts = [(partner[r], "rl%d" % r, oz[:])]
+        if r < 2:
+            parts.append((partner[r + 1], "ro%d" % (r + 1), T["oin%d" % (r + 1)][:]))
+        send_list([h_o], on[:], parts)
+        h_inv = scatter(r + 1, h_o)
+        k = 10
+        h = do("v", [h_inv, h_mk], V.tensor_tensor_scan, blk(sr, k), T.mk[:], T["inv%d" % (r + 1)][:], 0.0, A.mult, A.add)
+        h_back = do("v", [h, h_sc], V.tensor_scalar, blk(T["tb%d" % r], 9, K), sr[:, k * C + 15:(k + 1) * C:16],
+                    T.sc[:], HALF + 0.25, A.mult, A.add)
+        if r < 2:
+            st, steps = cycles(r + 1, h_inv, h_o)
+        else:
+            steps = []
+            hfo = do("s", [h_o], S.activation, T.fr[:], T.pc[:].indirect(on[:]), F.Identity, bias=float(HALF))
+            dma("y", [hfo], "sto", T.fo[:, :], T.fr[0:128:16, :])
+            h_vq = [do("v", [h_v], V.quantize_mx, T.vq[:], T.vs[:], T.vt[:])]
+        arr = ("rl%d" % r, len(topo.engines(partner[r], core)) // len(parts))
+        hz = []
+        he = [do("v", [hd[b]], V.tensor_copy, blk(fe, b), blk(fd, b)) for b in range(4)]
+        ha = [do("v", [arr, he[b]], V.tensor_tensor, blk(a, b), blk(fd, b).indirect(oz[:]), blk(fe, b), A.add)
+              for b in range(4)]
+        if r < 2 and CFG["jfirst"]:
+            steps[0]()
+        for b in range(4):
+            hz.append(do("s", [ha[b], arr], S.activation, z[:, b:4 * C:4], blk(a, b).indirect(oz[:]), F.Copy, scale=0.5))
+        hq = do("v", hz, V.quantize_mx, T["zq%d" % r][:], T["zs%d" % r][:], z[:])
+        at = 0
+        if r < 2:
+            at = CFG["pre"]
+            for s in steps[1 if CFG["jfirst"] else 0:at]:
+                s()
+        xn, rb = T["x%d" % (r + 1)], T["rb%d" % r]
+        hx = []
+        for b in range(4):
+            k = 1 + b if b < KEEP else 2 + b
+            hm = mm(k, T.wq, T.wp, 128 * b, T["zq%d" % r], T["zs%d" % r], [hq, h_w, h_p] + hd)
+            hr = do("s", [hm], S.activation, blk(rb, b), bank(k), F.Copy, scale=0.03125)
+            at_home = blk(rb, b).indirect(blk(T["tb%d" % r], 9, K))
+            if b < KEEP:
+                hx.append(do("v", [hr, h_back, hf[b]], V.tensor_tensor, xn[:, b:4 * C:4], at_home, blk(f, b), A.add))
+            else:
+                hs = T["hs%d" % r]
+                hr = do("s", [hr, h_back], S.activation, hs[:], at_home, F.Copy)
+                hx.append(do("v", [hr, h_pr[1 + b]], V.tensor_tensor, xn[:, b:4 * C:4], bank(1 + b), hs[:], A.add))
+        h_q = quant_x(r + 1, hx)
+    q, p = T.xq3, T.xs3
+    hy = [mm(i, T.vq, T.vs, 0, q, p, [h_q] + h_vq, i * HALF, (i + 1) * HALF) for i in range(2)]
+    h0 = do("v", [hy[0]], V.tensor_copy, T.ya[:, 0:HALF], bank(0, HALF))
+    h1 = do("s", [hy[1]], S.activation, T.ya[:, HALF:C], bank(1, HALF), F.Copy)
+    dma("y", [h_q], "sto", T.oc[:, :], q[:].bitcast(dt.uint8))
+    for i in range(4):
+        dma("y", [h_q], "sto", T.osc[4 * i:4 * i + 4, :], p[32 * i:32 * i + 4, :])
+    dma("y", [h0], "sto", T.y[:, 0:HALF], T.ya[:, 0:HALF])
+    dma("s", [h1], "sto", T.y[:, HALF:C], T.ya[:, HALF:C])
+    wait("g", list(done.items()))

@@ -1,4 +1,3 @@
-from concourse.bass import DstId, RemoteDMATransfer
 from concourse.mybir import dt, AluOpType, ActivationFunctionType
 
 C, K = 352, 22
@@ -6,13 +5,47 @@ HALF = 176
 BIG = 2.0 ** 30
 STEP = [1, 2, 4]
 NJ = 8
-CFG = {"pre": 2, "jfirst": True, "gap": [2, 3, 4], "dup": "-bvvvvvv"}
-KEEP = 3
+DUP = ["vvvvvvv", "vvvvvvv", "vvvvvvv"]
+HOME = ["vvvs", "vvvs", "vvssvvss"]
+TWIN = ["yyyy", "vyvy", "vvvv"]
+MEAN = ["sssh", "sssh", "sssh"]
+SIGN = ["v", "s", "s"]
+KEEP = ["ssss", "ssss", "ssss"]
+FAR = ["ssss", "ssss", "svsv"]
+OUT = ["ssss", "ssss", "svvs"]
+EARLY = [False, False, True]
+SPJ = [False, False, False]
+SPL = [False, False, False]
+SPT = [True, True, True]
+PARTS = [(0, 192), (192, C)]
+
+ORDER = """
+A g ul dd pc idn so0 si0 so1
+A y lod lu lx lv fe00 lp lw fe30 fe20 fe10
+A t ms0 mf00 mf30 mf20 mf10
+A v ones e uo o0 e0 e2 dm ma mb uq e3 mk16 row0 sc e1 eq n0 i0 uc q0
+A v s00 t00 l00 sign0 s10 t10 d10 of l10 s20 t20 d20 pa0 l20 s30 t30 d30 l30 s40 t40 d40 pb0 l40 s50 t50 d50 l50
+A v s60 t60 d60 l60 s70 d70 t70 l70 l80 s80 L80 t80 S80 vq T80 pc0 os0 OS0 om0 oa0 o1
+A s mk32 up mk64 mk128 mk256 mk j00 j10 f00 j20 j30 f30 j40 j50 f20 j60 f10 j70 place0 flag0 FLAG0 fcol0
+B g si+ sc sp xc+ xp+ sn+ so++
+B y fe1+ fe3+
+B t mr1 mr0 mr3 mr2 mf1+ ms+ mf2+ mf0+ md3+ md1+ md0+ md2+ mf3+
+B v a0 is im ia i+ a1 a2 a3 w3 zq pa+
+B v s0+ t0+ l0+ pb+ s1+ t1+ d1+ l1+ s2+ t2+ d2+ l2+ s3+ t3+ d3+ l3+ s4+ d4+ t4+
+B v x1 l4+ s5+ x0 d5+ t5+ x2 l5+ s6+ x3 t6+ d6+ q+ l6+
+B v s7+ d7+ t7+ l7+ l8+ s8+ L8+ t8+ S8+ pc+ T8+ fe2+ os+ fe0+ OS+ om+ oa+ o++
+B s z0 row+ z1 z2 z3 j0+ j1+ j2+ j3+ j4+
+B s r1 r0 j5+ r3 r2 h3 j6+ j7+ f1+ sign+ place+ f2+ f0+ flag+ FLAG+ f3+ fcol+
+C y fo oc0 oc1 osc1 osc0
+C t mr32 mr22 mr12 mr02 my0 my1
+C v is2 g32 im2 g12 ia2 ge32 ge02 ge12 ge22 a02 a22 a12 a32 w32 zq2 i3 r22 r12 x32 x12 x22 x02 x72 q3 x42 x62 x52 q4 ya1
+C s k02 g02 g22 fr k12 z02 z22 z12 z32 r32 h32 h22 r02 h72 h62 ya0 y0 osc3 osc2 y1
+"""
 
 SCRATCH = {
     "odl": ("sbuf", [128, K], "int32"), "pc": ("sbuf", [128, C], "bfloat16"),
-    "dd": ("sbuf", [128, C], "int32"), "dm": ("sbuf", [128, C], "int32"),
-    "ma": ("sbuf", [128, C], "float32"), "mb": ("sbuf", [128, C], "float32"),
+    "dd": ("sbuf", [128, 16], "int32"), "dm": ("sbuf", [128, 16], "int32"),
+    "ma": ("sbuf", [128, 16], "float32"), "mb": ("sbuf", [128, 16], "float32"),
     "mk": ("sbuf", [128, C], "bfloat16"), "sc": ("sbuf", [128, 1], "float32"),
     "ones": ("sbuf", [128, 128], "bfloat16"), "idn": ("sbuf", [128, 128], "bfloat16"),
     "et": ("sbuf", [128, 2048], "bfloat16"),
@@ -24,280 +57,308 @@ SCRATCH = {
     "vq": ("sbuf", [128, 128], "float8_e4m3fn_x4"), "vs": ("sbuf", [128, 128], "uint8"),
     "wq": ("sbuf", [128, 512], "float8_e4m3fn_x4"), "wp": ("sbuf", [128, 512], "uint8"),
     "ps": ("psum", [128, 4096], "float32"),
-    "ya": ("sbuf", [128, C], "float32"), "fr": ("sbuf", [128, C], "float32"),
+    "ya": ("sbuf", [128, C], "float32"), "fr": ("sbuf", [128, C], "float32"), "s0": ("sbuf", [128, C], "bfloat16"),
 }
 for _r in range(4):
     SCRATCH["x%d" % _r] = ("sbuf", [128, 4 * C], "bfloat16")
     SCRATCH["xq%d" % _r] = ("sbuf", [128, C], "float8_e4m3fn_x4")
     SCRATCH["xs%d" % _r] = ("sbuf", [128, C], "uint8")
-    SCRATCH["o%d" % _r] = ("sbuf", [128, K], "uint16")
-    SCRATCH["inv%d" % _r] = ("sbuf", [128, C], "bfloat16")
+    SCRATCH["o%d" % _r] = ("sbuf", [128, 2 * K], "uint16")
+    SCRATCH["of%d" % _r] = ("sbuf", [128, 2 * K], "float32")
 for _r in range(3):
-    SCRATCH["oin%d" % _r] = ("sbuf", [128, K], "uint16")
+    _d = "bfloat16"
+    SCRATCH["inv%d" % _r] = ("sbuf", [128, C], "bfloat16")
+    SCRATCH["oin%d" % _r] = ("sbuf", [128, 2 * K], "uint16")
     SCRATCH["f%d" % _r] = ("sbuf", [128, 4 * C], "bfloat16")
+    SCRATCH["fe%d" % _r] = ("sbuf", [128, 4 * C], "bfloat16")
     SCRATCH["a%d" % _r] = ("sbuf", [128, 4 * C], "float32")
     SCRATCH["z%d" % _r] = ("sbuf", [128, 4 * C], "bfloat16")
-    SCRATCH["rb%d" % _r] = ("sbuf", [128, 4 * C], "float32")
-    SCRATCH["hs%d" % _r] = ("sbuf", [128, C], "float32")
     SCRATCH["zq%d" % _r] = ("sbuf", [128, C], "float8_e4m3fn_x4")
     SCRATCH["zs%d" % _r] = ("sbuf", [128, C], "uint8")
-    SCRATCH["xi%d" % _r] = ("sbuf", [128, C], "float8_e4m3fn_x4")
-    SCRATCH["xp%d" % _r] = ("sbuf", [128, C], "uint8")
-    SCRATCH["fd%d" % _r] = ("sbuf", [128, 4 * C], "bfloat16")
-    SCRATCH["oz%d" % _r] = ("sbuf", [128, K], "uint16")
+    SCRATCH["zi%d" % _r] = ("sbuf", [128, C], "float8_e4m3fn_x4")
+    SCRATCH["zp%d" % _r] = ("sbuf", [128, C], "uint8")
+    SCRATCH["rb%d" % _r] = ("sbuf", [128, 4 * C], "float32")
+    SCRATCH["hs%d" % _r] = ("sbuf", [128, 4 * C], "float32")
     SCRATCH["jr%d" % _r] = ("sbuf", [128, NJ * C], "bfloat16")
-    SCRATCH["lr%d" % _r] = ("sbuf", [128, 9 * C], "bfloat16")
-    SCRATCH["le%d" % _r] = ("sbuf", [128, NJ * C], "bfloat16")
-    SCRATCH["fe%d" % _r] = ("sbuf", [128, 4 * C], "bfloat16")
+    SCRATCH["lr%d" % _r] = ("sbuf", [128, 9 * C], _d)
+    SCRATCH["le%d" % _r] = ("sbuf", [128, NJ * C], _d)
     SCRATCH["sr%d" % _r] = ("sbuf", [128, 11 * C], "bfloat16")
-    SCRATCH["tb%d" % _r] = ("sbuf", [128, 10 * K], "uint16")
-    SCRATCH["sg%d" % _r] = ("sbuf", [128, 3 * C], "bfloat16")
+    SCRATCH["tb%d" % _r] = ("sbuf", [128, 9 * K], "uint16")
+    SCRATCH["sg%d" % _r] = ("sbuf", [128, 4 * C], "bfloat16")
     SCRATCH["sm%d" % _r] = ("sbuf", [128, 8 * K], "float32")
+    if EARLY[_r]:
+        SCRATCH["fd%d" % _r] = ("sbuf", [128, 4 * C], "bfloat16")
+        SCRATCH["oz%d" % _r] = ("sbuf", [128, K], "uint16")
 SEMAPHORES = (["sv", "ss", "st", "sg", "loc", "sto"] + ["l" + n for n in ("od", "x", "u", "v", "w", "p")]
-              + [n + str(r) for n in ("ro", "rx", "rl") for r in range(3)])
+              + [n + str(r) for n in ("ro", "ri", "rz") for r in range(3)]
+              + ["fe%d%d" % (b, r) for b in range(4) for r in range(3) if TWIN[r][b] == "y"]
+              + ["rn%d" % r for r in range(3) if EARLY[r]])
+OWN = {"v": "sv", "s": "ss", "t": "st", "g": "sg"}
 
 
-def rank_program(g, core, T, topo):
+def plan(g, core, T, topo):
     rank = T.rank_of(core)
-    if rank is None:
-        return
     A, F = AluOpType, ActivationFunctionType
-    Q = {"v": g.vector, "s": g.scalar, "t": g.tensor, "g": g, "y": g.sync}
-    own = {"v": "sv", "s": "ss", "t": "st", "g": "sg"}
-    done, seen = {}, {}
+    V, S, PE, Y = g.vector, g.scalar, g.tensor, g.sync
+    calls = {}
+    partner = [T.cores[rank ^ s] for s in STEP]
 
-    def wait(q, after):
-        need = {}
-        for h in after:
-            if h is not None:
-                need[h[0]] = max(need.get(h[0], 0), h[1])
-        for name, n in need.items():
-            if seen.get((q, name), 0) < n:
-                Q[q].wait_ge(T.sem[name], n)
-                seen[(q, name)] = n
+    def do(name, q, after, call, *args, **kw):
+        calls[name] = (q, after, (OWN[q], 1), lambda: call(*args, **kw).then_inc(T.sem[OWN[q]], 1))
 
-    def do(q, after, call, *args, **kw):
-        wait(q, after)
-        s = own[q]
-        call(*args, **kw).then_inc(T.sem[s], 1)
-        done[s] = done.get(s, 0) + 1
-        return (s, done[s])
+    def dma(name, q, after, s, out, in_):
+        calls[name] = (q, after, (s, 16), lambda: {"y": Y, "s": S}[q].dma_start(out, in_).then_inc(T.sem[s], 16))
 
-    def dma(q, after, s, out, in_):
-        wait(q, after)
-        Q[q].dma_start(out, in_).then_inc(T.sem[s], 16)
-        done[s] = done.get(s, 0) + 16
-        return (s, done[s])
-
-    def send(after, dst, s, out, in_):
-        wait("g", after)
+    def send(name, after, dst, s, out, in_):
         rid, pid = topo.addr(dst)[:2]
-        g.remote_dma(out, in_, T.sem[s], T.sem["loc"], pid, rid, topo.mask(core, dst))
-        done["loc"] = done.get("loc", 0) + len(topo.engines(core, dst))
+        calls[name] = ("g", after, ("loc", len(topo.engines(core, dst))),
+                       lambda: g.remote_dma(out, in_, T.sem[s], T.sem["loc"], pid, rid, topo.mask(core, dst)))
 
-    def send_list(after, src, parts):
-        wait("g", after)
-        n = len(topo.engines(core, parts[0][0])) // len(parts)
-        tr = []
-        for i, (dst, s, out) in enumerate(parts):
-            rid, pid = topo.addr(dst)[:2]
-            m = sum(1 << e for e in topo.engines(core, dst)[n * i:n * i + n])
-            tr.append(RemoteDMATransfer(dst_ids=[DstId(rid=rid, pnc=pid)], dma_engine_mask=m, remote_sem=T.sem[s], src=src, dst=out))
-        g.remote_dma_fused(tr, local_sem=T.sem["loc"])
-        done["loc"] = done.get("loc", 0) + n * len(parts)
-
-    V, S, PE = g.vector, g.scalar, g.tensor
+    def landed(s, r, *names):
+        return (s + str(r), len(names) * len(topo.engines(partner[r], core)), names)
 
     def blk(t, b, n=C):
         return t[:, b * n:(b + 1) * n]
 
-    def bank(k, n=C):
-        return T.ps[:, 512 * k:512 * k + n]
+    def bank(k, lo=0, hi=C):
+        return T.ps[:, 512 * k + lo:512 * k + hi]
 
-    partner = [T.cores[rank ^ s] for s in STEP]
-    h_od = dma("y", [], "lod", T.odl[:], T.od[:, :])
-    h_x = dma("s", [], "lx", T.x0[:], T.x[:, :])
-    h_u = dma("y", [], "lu", T.ut[:], T.u[:, :])
-    h_w = dma("y", [], "lw", T.wq[:].bitcast(dt.uint8), T.wc[:, :])
-    h_p = dma("y", [], "lp", T.wp[:], T.ws[:, :])
-    h_v = dma("s", [], "lv", T.vt[:], T.v[:, :])
-    h_pc = do("g", [], g.iota, T.pc[:], [[1, C]], -HALF, 0, allow_small_or_imprecise_dtypes=True)
-    h_dd = do("g", [], g.iota, T.dd[:], [[1, C]], 128, -1)
-    h_ul = do("g", [], g.iota, T.ul[:], [[16, 8]], 0, 0)
-    h_one = do("v", [], V.memset, T.ones[:], 1.0)
-    h_e0 = do("v", [], V.memset, T.et[:], 0.0)
-    h_o = do("v", [h_od], V.tensor_copy, T.o0[:], T.odl[:])
-    send([h_o], partner[0], "ro0", T.oin0[:], T.o0[:])
-    h_id = do("g", [h_one], g.affine_select, T.idn[:], T.ones[:], [[-1, 128]], A.is_equal, 0.0, 0, 1)
+    def mm(name, after, k, a, ap, ca, b, bp, lo=0, hi=C):
+        do(name, "t", after, PE.matmul_mx, bank(k, 0, hi - lo), a[:, ca:ca + 128], ap[:, ca:ca + 128],
+           b[:, lo:hi], bp[:, lo:hi], True, True)
 
-    def scatter(r, h_o):
-        return do("v", [h_o, h_pc], V.tensor_copy, T["inv%d" % r][:].indirect(T["o%d" % r][:]), T.pc[:])
+    def scan(name, after, out, k, rows, i, lo=0, hi=C):
+        do(name, "v", after + ["mk"], V.tensor_tensor_scan, out[:, k * C + lo:k * C + hi], T.mk[:, lo:hi],
+           rows[:, i * C + lo:i * C + hi], 0.0, A.mult, A.add)
 
-    h_inv = scatter(0, h_o)
-    h_dm = do("v", [h_dd], V.tensor_scalar, T.dm[:], T.dd[:], 15, None, A.bitwise_and)
-    h_sc = do("v", [h_dm], V.tensor_scalar, T.sc[:], T.dm[:, 0:1], 1, 1.0 / BIG, A.is_equal, A.max)
-    h_ma = do("v", [h_dm], V.tensor_scalar, T.ma[:], T.dm[:], 1, BIG, A.is_equal, A.mult)
-    h_mb = do("v", [h_dm], V.tensor_scalar, T.mb[:], T.dm[:], 2, None, A.is_ge)
-    h_mk = do("v", [h_ma, h_mb], V.tensor_tensor, T.mk[:], T.ma[:], T.mb[:], A.add)
-    h_et = [do("v", [h_e0, h_id], V.tensor_copy, T.et[:, 512 * b + b:512 * (b + 1):4], T.idn[:]) for b in range(4)]
-    h_uo = do("v", [h_ul], V.tensor_copy, T.uo[:], T.ul[:])
-    h_uq = do("v", [h_u], V.quantize_mx, T.uq[:], T.us[:], T.ut[:])
-    h_eq = do("v", h_et, V.quantize_mx, T.eq[:], T.es[:], T.et[:])
-    h_u2 = do("v", [h_uq, h_uo], V.tensor_copy, T.u2q[:].bitcast(dt.uint32),
-              T.uq[:].bitcast(dt.uint32).indirect(T.uo[:]))
-    h_u3 = do("v", [h_uq, h_uo], V.tensor_copy, T.u2s[:], T.us[:].indirect(T.uo[:]))
-    h_vq = []
+    def ends(t, k, lo=0, hi=C):
+        return t[:, k * C + lo + 15:k * C + hi:16]
 
-    def quant_x(r, after):
-        return do("v", after, V.quantize_mx, T["xq%d" % r][:], T["xs%d" % r][:], T["x%d" % r][:])
+    def table(name, after, out, t, k, lo=0, hi=C):
+        do(name, "v", after + ["sc"], V.tensor_scalar, out, ends(t, k, lo, hi), T.sc[:], HALF + 0.25, A.mult, A.add)
 
-    def mm(k, a, ap, ca, b, bp, after, lo=0, hi=C):
-        return do("t", after, PE.matmul_mx, bank(k, hi - lo), a[:, ca:ca + 128], ap[:, ca:ca + 128],
-                  b[:, lo:hi], bp[:, lo:hi], True, True)
-
-    def table(r, k, row, after):
-        sr = blk(T["sr%d" % r], k)
-        h = do("v", after + [h_mk], V.tensor_tensor_scan, sr, T.mk[:], row, 0.0, A.mult, A.add)
-        return do("v", [h, h_sc], V.tensor_scalar, blk(T["tb%d" % r], k, K),
-                  T["sr%d" % r][:, k * C + 15:(k + 1) * C:16], T.sc[:], HALF + 0.25, A.mult, A.add)
-
-    def products(r, h_q):
-        q, p = T["xq%d" % r], T["xs%d" % r]
-        hs = mm(0, T.u2q, T.u2s, 0, q, p, [h_q, h_u2, h_u3])
-        return [hs] + [mm(1 + b, T.eq, T.es, 128 * b, q, p, [h_q, h_eq]) for b in range(4)]
-
-    def cycles(r, h_inv, h_o):
-        tb, jr, lr, l2, inv, oin = (T[n + str(r)] for n in ("tb", "jr", "lr", "le", "inv", "oin"))
-        arr = ("ro%d" % r, len(topo.engines(partner[r], core)) // (1 if r == 0 else 2))
-        st = {}
-
-        def first():
-            st["j"] = do("s", [arr, h_inv], S.activation, blk(jr, 0), inv[:].indirect(oin[:]), F.Copy)
-            st["l"] = do("v", [arr, h_inv, h_pc], V.tensor_tensor, blk(lr, 0), inv[:].indirect(oin[:]), T.pc[:], A.min)
-            st["t"] = table(r, 0, blk(jr, 0), [st["j"]])
-
-        def step(k):
-            def f():
-                hj = do("s", [st["t"], st["j"]], S.activation, blk(jr, k), blk(jr, k - 1).indirect(blk(tb, k - 1, K)), F.Copy)
-                if k == 1:
-                    prep()
-                if CFG["dup"][k] == "s":
-                    h2 = do("s", [st["l"]], S.activation, blk(l2, k), blk(lr, k - 1), F.Copy)
-                if CFG["dup"][k] == "b":
-                    h2 = do("v", [st["l"]], V.tensor_copy, blk(l2, k), blk(lr, k - 1))
-                ht = table(r, k, blk(jr, k), [hj])
-                if CFG["dup"][k] == "v":
-                    h2 = do("v", [st["l"]], V.tensor_copy, blk(l2, k), blk(lr, k - 1))
-                st["l"] = do("v", [ht, st["l"], h2], V.tensor_tensor, blk(lr, k), blk(lr, k - 1).indirect(blk(tb, k, K)), blk(l2, k), A.min)
-                st["j"], st["t"] = hj, ht
-            return f
-
-        def prep():
-            sm, o = T["sm%d" % r], T["o%d" % r]
-            h1 = do("v", [arr, h_sc], V.tensor_scalar, blk(sm, 0, K), oin[:], T.sc[:], None, A.mult)
-            h2 = do("v", [h_o, h_sc], V.tensor_scalar, blk(sm, 1, K), o[:], T.sc[:], None, A.mult)
-            h3 = do("v", [h_o], V.tensor_scalar, blk(sm, 2, K), o[:], 0.25, None, A.add)
-            h4 = do("v", [h1, h2], V.tensor_tensor, blk(sm, 3, K), blk(sm, 0, K), blk(sm, 1, K), A.subtract)
-            st["prep"] = [h3, h4]
-
-        def last():
-            st["l"] = do("v", [st["t"], st["l"]], V.tensor_tensor, blk(lr, 8), blk(lr, 7).indirect(blk(tb, 7, K)), blk(lr, 6), A.min)
-            st["leader"] = table(r, 8, blk(lr, 8), [st["l"]])
-        return st, [first] + [step(k) for k in range(1, NJ)] + [last]
-
-    h_q = quant_x(0, [h_x])
-    st, steps = cycles(0, h_inv, h_o)
-    steps[0]()
-    at = 1
-    for r in range(3):
-        o, on = T["o%d" % r], T["o%d" % (r + 1)]
-        f, fd, fe, sg, a, z, oz = (T[n + str(r)] for n in ("f", "fd", "fe", "sg", "a", "z", "oz"))
-        send([h_q], partner[r], "rx%d" % r, T["xi%d" % r][:].bitcast(dt.uint8), T["xq%d" % r][:].bitcast(dt.uint8))
-        send([h_q], partner[r], "rx%d" % r, T["xp%d" % r][:], T["xs%d" % r][:])
-        h_pr = products(r, h_q)
-        hf = [None] * 4
-        arr = ("rx%d" % r, 2 * len(topo.engines(partner[r], core)))
-
-        def fcopy(q, b):
-            if q == "v":
-                hf[b] = do("v", [h_pr[1 + b]], V.tensor_copy, blk(f, b), bank(1 + b))
-            else:
-                hf[b] = do("s", [h_pr[1 + b]], S.activation, blk(f, b), bank(1 + b), F.Copy)
-        rest = steps[at:]
-        sign = lambda: do("s", [h_pr[0]], S.activation, blk(sg, 0), bank(0), F.Sign)
-        place = lambda h: do("s", [h, h_o], S.activation, blk(sg, 1), blk(sg, 0).indirect(o[:]), F.Relu)
-        gap = CFG["gap"]
-        for i, s in enumerate(rest):
-            if i == len(rest) - 1:
-                hs = place(sign())
-            s()
-            if i in gap:
-                fcopy("s", gap.index(i))
-        hfl = do("s", [hs, st["leader"]], S.activation, blk(sg, 2), blk(sg, 1).indirect(blk(T["tb%d" % r], 8, K)), F.Copy)
-        hd = []
-        for b in range(4):
-            hm = mm((5 + b) % 8, T.eq, T.es, 128 * b, T["xi%d" % r], T["xp%d" % r], [arr, h_eq, hs])
-            hd.append(do("s", [hm], S.activation, blk(fd, b), bank((5 + b) % 8), F.Copy))
-        for b in range(KEEP):
-            if hf[b] is None:
-                fcopy("s", b)
-        sr, sm = T["sr%d" % r], T["sm%d" % r]
-        h = do("v", [hfl, h_mk], V.tensor_tensor_scan, blk(sr, 9), T.mk[:], blk(sg, 2), 0.0, A.mult, A.add)
-        h = do("v", [h] + st["prep"], V.tensor_tensor, blk(sm, 4, K), sr[:, 9 * C + 15:10 * C:16], blk(sm, 3, K), A.mult)
-        h = do("v", [h], V.tensor_tensor, blk(sm, 5, K), blk(sm, 4, K), blk(sm, 2, K), A.add)
-        h_o = do("v", [h], V.tensor_copy, on[:], blk(sm, 5, K))
-        parts = [(partner[r], "rl%d" % r, oz[:])]
-        if r < 2:
-            parts.append((partner[r + 1], "ro%d" % (r + 1), T["oin%d" % (r + 1)][:]))
-        send_list([h_o], on[:], parts)
-        h_inv = scatter(r + 1, h_o)
-        k = 10
-        h = do("v", [h_inv, h_mk], V.tensor_tensor_scan, blk(sr, k), T.mk[:], T["inv%d" % (r + 1)][:], 0.0, A.mult, A.add)
-        h_back = do("v", [h, h_sc], V.tensor_scalar, blk(T["tb%d" % r], 9, K), sr[:, k * C + 15:(k + 1) * C:16],
-                    T.sc[:], HALF + 0.25, A.mult, A.add)
-        if r < 2:
-            st, steps = cycles(r + 1, h_inv, h_o)
+    def again(name, q, after, out, in_):
+        if q == "s":
+            do(name, q, after, S.activation, out, in_, F.Copy)
+        elif q == "v":
+            do(name, q, after, V.tensor_copy, out, in_)
         else:
-            steps = []
-            hfo = do("s", [h_o], S.activation, T.fr[:], T.pc[:].indirect(on[:]), F.Identity, bias=float(HALF))
-            dma("y", [hfo], "sto", T.fo[:, :], T.fr[0:128:16, :])
-            h_vq = [do("v", [h_v], V.quantize_mx, T.vq[:], T.vs[:], T.vt[:])]
-        arr = ("rl%d" % r, len(topo.engines(partner[r], core)) // len(parts))
-        hz = []
-        he = [do("v", [hd[b]], V.tensor_copy, blk(fe, b), blk(fd, b)) for b in range(4)]
-        ha = [do("v", [arr, he[b]], V.tensor_tensor, blk(a, b), blk(fd, b).indirect(oz[:]), blk(fe, b), A.add)
-              for b in range(4)]
-        if r < 2 and CFG["jfirst"]:
-            steps[0]()
+            do(name, q, after, g.affine_select, out, in_, [[0, C]], A.is_ge, 0.0, 0, 0)
+
+    dma("lod", "y", [], "lod", T.odl[:], T.od[:, :])
+    dma("lx", "y", [], "lx", T.x0[:], T.x[:, :])
+    dma("lu", "y", [], "lu", T.ut[:], T.u[:, :])
+    dma("lw", "y", [], "lw", T.wq[:].bitcast(dt.uint8), T.wc[:, :])
+    dma("lp", "y", [], "lp", T.wp[:], T.ws[:, :])
+    dma("lv", "y", [], "lv", T.vt[:], T.v[:, :])
+    do("dd", "g", [], g.iota, T.dd[:], [[1, 16]], 128, -1)
+    do("ul", "g", [], g.iota, T.ul[:], [[16, 8]], 0, 0)
+    do("ones", "v", [], V.memset, T.ones[:], 1.0)
+    do("idn", "g", ["ones"], g.affine_select, T.idn[:], T.ones[:], [[-1, 128]], A.is_equal, 0.0, 0, 1)
+    do("pc", "g", [], g.iota, T.pc[:], [[1, C]], -HALF, 0, allow_small_or_imprecise_dtypes=True)
+    do("e", "v", [], V.memset, T.et[:], 0.0)
+    do("dm", "v", ["dd"], V.tensor_scalar, T.dm[:], T.dd[:], 15, None, A.bitwise_and)
+    do("sc", "v", ["dm"], V.tensor_scalar, T.sc[:], T.dm[:, 0:1], 1, 1.0 / BIG, A.is_equal, A.max)
+    do("ma", "v", ["dm"], V.tensor_scalar, T.ma[:], T.dm[:], 1, BIG, A.is_equal, A.mult)
+    do("mb", "v", ["dm"], V.tensor_scalar, T.mb[:], T.dm[:], 2, None, A.is_ge)
+    do("mk16", "v", ["ma", "mb"], V.tensor_tensor, T.mk[:, 0:16], T.ma[:], T.mb[:], A.add)
+    for n in (16, 32, 64, 128, 256):
+        m = min(n, C - n)
+        do("mk%d" % (n + m) if n + m < C else "mk", "s", ["mk%d" % n], S.activation, T.mk[:, n:n + m], T.mk[:, 0:m], F.Copy)
+    for b in range(4):
+        do("e%d" % b, "v", ["e", "idn"], V.tensor_copy, T.et[:, 512 * b + b:512 * (b + 1):4], T.idn[:])
+    do("eq", "v", ["e0", "e1", "e2", "e3"], V.quantize_mx, T.eq[:], T.es[:], T.et[:])
+    do("uo", "v", ["ul"], V.tensor_copy, T.uo[:], T.ul[:])
+    do("uq", "v", ["lu"], V.quantize_mx, T.uq[:], T.us[:], T.ut[:])
+    do("uc", "v", ["uq", "uo"], V.tensor_copy, T.u2q[:].bitcast(dt.uint32), T.uq[:].bitcast(dt.uint32).indirect(T.uo[:]))
+    do("up", "s", ["uq", "uo"], S.activation, T.u2s[:], T.us[:].indirect(T.uo[:]), F.Copy)
+    do("vq", "v", ["lv"], V.quantize_mx, T.vq[:], T.vs[:], T.vt[:])
+    do("o0", "v", ["lod"], V.tensor_copy, blk(T.o0, 0, K), T.odl[:])
+    do("row0", "v", ["o0", "pc"], V.tensor_copy, T.inv0[:].indirect(blk(T.o0, 0, K)), T.pc[:])
+    scan("n0", ["row0"], T.s0, 0, T.inv0, 0)
+    table("i0", ["n0"], blk(T.o0, 1, K), T.s0, 0)
+    do("of", "v", ["o0", "i0"], V.tensor_scalar, T.of0[:], T.o0[:], 0.25, None, A.add)
+    do("q0", "v", ["lx"], V.quantize_mx, T.xq0[:], T.xs0[:], T.x0[:])
+
+    for r in range(3):
+        def n(s, r=r):
+            return s + str(r)
+        o, on, of, ofn = T[n("o")], T[n("o", r + 1)], T[n("of")], T[n("of", r + 1)]
+        oin, inv, tb, jr, lr, le, sr, sg, sm = (T[n(s)] for s in ("oin", "inv", "tb", "jr", "lr", "le", "sr", "sg", "sm"))
+        f, fe, a, z, rb, hs, xn = T[n("f")], T[n("fe")], T[n("a")], T[n("z")], T[n("rb")], T[n("hs")], T[n("x", r + 1)]
+        xq, xs, zq, zs, zi, zp = (T[n(s)] for s in ("xq", "xs", "zq", "zs", "zi", "zp"))
+        send(n("so"), [n("o")], partner[r], n("ro"), blk(oin, 0, K), blk(o, 0, K))
+        send(n("si"), [n("i")], partner[r], n("ri"), blk(oin, 1, K), blk(o, 1, K))
+        there = landed("ro", r, n("so"))
+        sent = ("xc", "xp") if EARLY[r] else ("sc", "sp")
+        codes = landed("rz", r, n(sent[0]), n(sent[1]))
+        parts = PARTS if r == 2 else [(0, C)]
+        mm(n("ms"), [n("q"), "uc", "up"], 0, T.u2q, T.u2s, 0, xq, xs)
+        if SIGN[r] == "s":
+            do(n("sign"), "s", [n("ms")], S.activation, blk(sg, 0), bank(0), F.Sign)
+        else:
+            do(n("sign"), "v", [n("ms")], V.tensor_scalar, blk(sg, 0), bank(0), 0.0, None, A.is_gt)
+        do(n("place"), "s", [n("sign"), n("o")], S.activation, blk(sg, 1), blk(sg, 0).indirect(blk(o, 0, K)), F.Relu)
+        kept, twin = [], []
         for b in range(4):
-            hz.append(do("s", [ha[b], arr], S.activation, z[:, b:4 * C:4], blk(a, b).indirect(oz[:]), F.Copy, scale=0.5))
-        hq = do("v", hz, V.quantize_mx, T["zq%d" % r][:], T["zs%d" % r][:], z[:])
-        at = 0
-        if r < 2:
-            at = CFG["pre"]
-            for s in steps[1 if CFG["jfirst"] else 0:at]:
-                s()
-        xn, rb = T["x%d" % (r + 1)], T["rb%d" % r]
-        hx = []
-        for b in range(4):
-            k = 1 + b if b < KEEP else 2 + b
-            hm = mm(k, T.wq, T.wp, 128 * b, T["zq%d" % r], T["zs%d" % r], [hq, h_w, h_p] + hd)
-            hr = do("s", [hm], S.activation, blk(rb, b), bank(k), F.Copy, scale=0.03125)
-            at_home = blk(rb, b).indirect(blk(T["tb%d" % r], 9, K))
-            if b < KEEP:
-                hx.append(do("v", [hr, h_back, hf[b]], V.tensor_tensor, xn[:, b:4 * C:4], at_home, blk(f, b), A.add))
+            mm(n("mf%d" % b), [n("q"), "eq"], 1 + b, T.eq, T.es, 128 * b, xq, xs)
+            kept.append(n("mf%d" % b))
+            if not EARLY[r] or "v" in HOME[r][b::4]:
+                kept[b] = n(("k%d" if EARLY[r] else "f%d") % b)
+                again(kept[b], KEEP[r][b], [n("mf%d" % b)], blk(f, b), bank(1 + b))
+            if EARLY[r]:
+                k = (5 + b) % 8
+                mm(n("md%d" % b), [codes, "eq", n("sign")], k, T.eq, T.es, 128 * b, zi, zp)
+                again(n("g%d" % b), FAR[r][b], [n("md%d" % b)], blk(T[n("fd")], b), bank(k))
+            first, row = (n("g%d" % b), blk(T[n("fd")], b)) if EARLY[r] else (n("f%d" % b), blk(f, b))
+            twin.append(n(("ge%d" if EARLY[r] else "fe%d") % b))
+            if TWIN[r][b] == "y":
+                dma(twin[b], "y", [first], n("fe%d" % b), blk(fe, b), row)
             else:
-                hs = T["hs%d" % r]
-                hr = do("s", [hr, h_back], S.activation, hs[:], at_home, F.Copy)
-                hx.append(do("v", [hr, h_pr[1 + b]], V.tensor_tensor, xn[:, b:4 * C:4], bank(1 + b), hs[:], A.add))
-        h_q = quant_x(r + 1, hx)
+                again(twin[b], TWIN[r][b], [first], blk(fe, b), row)
+        def runs(split):
+            return [(str.lower, *PARTS[0]), (str.upper, *PARTS[1])] if split else [(str.lower, 0, C)]
+
+        def both(s, k, split, r=r):
+            return [case(s) + str(k) + str(r) for case, lo, hi in runs(split)]
+
+        def row(t, k, lo, hi):
+            return t[:, k * C + lo:k * C + hi]
+
+        def tab(t, k, lo, hi):
+            return t[:, k * K + lo // 16:k * K + hi // 16]
+
+        def tables(k, split, h):
+            return both("t", k, sj)[h:h + 1] if split and sj else both("t", k, sj)
+
+        sj, sl, st = SPJ[r], SPL[r], SPT[r]
+        for k in range(NJ):
+            for h, (case, lo, hi) in enumerate(runs(sj)):
+                if k:
+                    do(n(case("j%d" % k)), "s", both("j", k - 1, sj) + tables(k - 1, sj, h), S.activation,
+                       row(jr, k, lo, hi), blk(jr, k - 1).indirect(tab(tb, k - 1, lo, hi)), F.Copy)
+                else:
+                    do(n(case("j0")), "s", [there, n("row")], S.activation, row(jr, 0, lo, hi), inv[:].indirect(tab(oin, 0, lo, hi)), F.Copy)
+                scan(n(case("s%d" % k)), [n(case("j%d" % k))], sr, k, jr, k, lo, hi)
+                table(n(case("t%d" % k)), [n(case("s%d" % k))], tab(tb, k, lo, hi), sr, k, lo, hi)
+            for h, (case, lo, hi) in enumerate(runs(sl)):
+                if k:
+                    again(n(case("d%d" % k)), DUP[r][k - 1], [n(case("l%d" % (k - 1)))], row(le, k, lo, hi), row(lr, k - 1, lo, hi))
+                    do(n(case("l%d" % k)), "v", both("l", k - 1, sl) + tables(k, sl, h) + [n(case("d%d" % k))], V.tensor_tensor,
+                       row(lr, k, lo, hi), blk(lr, k - 1).indirect(tab(tb, k, lo, hi)), row(le, k, lo, hi), A.min)
+                else:
+                    do(n(case("l0")), "v", [there, n("row"), "pc"], V.tensor_tensor,
+                       row(lr, 0, lo, hi), inv[:].indirect(tab(oin, 0, lo, hi)), T.pc[:, lo:hi], A.min)
+        for case, lo, hi in runs(st):
+            do(n(case("l8")), "v", both("l", 7, sl), V.tensor_tensor,
+               row(lr, 8, lo, hi), blk(lr, 7).indirect(tab(tb, 7, lo, hi)), row(lr, 6, lo, hi), A.min)
+            scan(n(case("s8")), [n(case("l8"))], sr, 8, lr, 8, lo, hi)
+            table(n(case("t8")), [n(case("s8"))], tab(tb, 8, lo, hi), sr, 8, lo, hi)
+            do(n(case("flag")), "s", [n("place"), n(case("t8"))], S.activation,
+               row(sg, 2, lo, hi), blk(sg, 1).indirect(tab(tb, 8, lo, hi)), F.Copy)
+            scan(n(case("os")), [n(case("flag"))], sr, 9, sg, 2, lo, hi)
+        do(n("pa"), "v", [there, landed("ri", r, n("si"))], V.tensor_scalar, blk(sm, 0, 2 * K), oin[:], 0.25, None, A.add)
+        do(n("pb"), "v", [n("pa")] + (["of"] if r == 0 else [n("oa", r - 1), n("ia", r - 1)]), V.tensor_tensor,
+           blk(sm, 1, 2 * K), blk(sm, 0, 2 * K), of[:], A.subtract)
+        do(n("pc"), "v", [n("pb"), "sc"], V.tensor_scalar, blk(sm, 2, 2 * K), blk(sm, 1, 2 * K), T.sc[:], None, A.mult)
+        do(n("fcol"), "s", both("flag", "", st) + [n("i")], S.activation, blk(sg, 3), blk(sg, 2).indirect(blk(o, 1, K)), F.Copy)
+        scan(n("is"), [n("fcol")], sr, 10, sg, 3)
+        for h, s in enumerate("oi"):
+            do(n(s + "m"), "v", both(s + "s", "", st and h == 0) + [n("pc")], V.tensor_tensor,
+               blk(sm, 6 + h, K), ends(sr, 9 + h), blk(sm, 4 + h, K), A.mult)
+            do(n(s + "a"), "v", [n(s + "m")], V.tensor_tensor, blk(ofn, h, K), blk(sm, 6 + h, K), blk(of, h, K), A.add)
+            do(n(s, r + 1), "v", [n(s + "a")], V.tensor_copy, blk(on, h, K), blk(ofn, h, K))
+        if r < 2:
+            do(n("row", r + 1), "s", [n("i", r + 1), "pc"], S.activation, T[n("inv", r + 1)][:], T.pc[:].indirect(blk(on, 1, K)), F.Copy)
+        if EARLY[r]:
+            send(n("sn"), [n("o", r + 1)], partner[r], n("rn"), T[n("oz")][:], blk(on, 0, K))
+            by, known, d, out, made = T[n("oz")], landed("rn", r, n("sn")), T[n("fd")], (xq, xs), n("q")
+        else:
+            by, known, d, out, made = on, n("o", r + 1), f, (zq, zs), n("zq")
+        means = []
+        for b in range(4):
+            do(n("a%d" % b), "v", [known, twin[b]], V.tensor_tensor, blk(a, b), blk(d, b).indirect(by[:, 0:K]), blk(fe, b), A.add)
+            lo = PARTS[1][0] if MEAN[r][b] == "h" else C
+            do(n("z%d" % b), "s", [n("a%d" % b), known], S.activation, z[:, b:4 * lo:4], blk(a, b).indirect(by[:, 0:lo // 16]), F.Copy, scale=0.5)
+            means.append(n("z%d" % b))
+            if lo < C:
+                do(n("w%d" % b), "v", [n("a%d" % b)], V.tensor_scalar, z[:, 4 * lo + b:4 * C:4], blk(a, b).indirect(by[:, lo // 16:K]), 0.5, None, A.mult)
+                means.append(n("w%d" % b))
+        do(n("zq"), "v", means, V.quantize_mx, zq[:], zs[:], z[:])
+        send(n(sent[0]), [made], partner[r], n("rz"), zi[:].bitcast(dt.uint8), out[0][:].bitcast(dt.uint8))
+        send(n(sent[1]), [made], partner[r], n("rz"), zp[:], out[1][:])
+        for b in range(4):
+            k = (5 + b) % 8
+            if EARLY[r]:
+                mm(n("mr%d" % b), [n("zq"), "lw", "lp"], k, T.wq, T.wp, 128 * b, zq, zs)
+            else:
+                mm(n("mr%d" % b), [codes, "lw", "lp", n("sign")], k, T.wq, T.wp, 128 * b, zi, zp)
+            if OUT[r][b] == "s":
+                do(n("r%d" % b), "s", [n("mr%d" % b)], S.activation, blk(rb, b), bank(k), F.Copy, scale=0.03125)
+            else:
+                do(n("r%d" % b), "v", [n("mr%d" % b)], V.tensor_scalar, blk(rb, b), bank(k), 0.03125, None, A.mult)
+            for h, (lo, hi) in enumerate(parts):
+                at_home, i = blk(rb, b).indirect(on[:, K + lo // 16:K + hi // 16]), b + 4 * h
+                to = xn[:, 4 * lo + b:4 * hi:4]
+                if HOME[r][i] == "v":
+                    do(n("x%d" % i), "v", [n("r%d" % b), n("i", r + 1), kept[b]], V.tensor_tensor, to, at_home, f[:, b * C + lo:b * C + hi], A.add)
+                else:
+                    do(n("h%d" % i), "s", [n("r%d" % b), n("i", r + 1)], S.activation, hs[:, b * C + lo:b * C + hi], at_home, F.Copy)
+                    do(n("x%d" % i), "v", [n("h%d" % i), kept[b]], V.tensor_tensor, to, bank(1 + b, lo, hi), hs[:, b * C + lo:b * C + hi], A.add)
+        for h, (lo, hi) in enumerate(parts):
+            do(n("q", r + 1 + h), "v", [n("x%d" % (b + 4 * h)) for b in range(4)], V.quantize_mx,
+               T[n("xq", r + 1)][:, lo:hi], T[n("xs", r + 1)][:, lo:hi], xn[:, 4 * lo:4 * hi])
+    do("fr", "s", ["o3", "pc"], S.activation, T.fr[:], T.pc[:].indirect(blk(T.o3, 0, K)), F.Identity, bias=float(HALF))
+    dma("fo", "y", ["fr"], "sto", T.fo[:, :], T.fr[0:128:16, :])
     q, p = T.xq3, T.xs3
-    hy = [mm(i, T.vq, T.vs, 0, q, p, [h_q] + h_vq, i * HALF, (i + 1) * HALF) for i in range(2)]
-    h0 = do("v", [hy[0]], V.tensor_copy, T.ya[:, 0:HALF], bank(0, HALF))
-    h1 = do("s", [hy[1]], S.activation, T.ya[:, HALF:C], bank(1, HALF), F.Copy)
-    dma("y", [h_q], "sto", T.oc[:, :], q[:].bitcast(dt.uint8))
+    for h, (lo, hi) in enumerate(PARTS):
+        mm("my%d" % h, ["q%d" % (3 + h), "vq", "r02", "r12"], 5 + h, T.vq, T.vs, 0, q, p, lo, hi)
+        again("ya%d" % h, "sv"[h], ["my%d" % h], T.ya[:, lo:hi], bank(5 + h, 0, hi - lo))
+        dma("oc%d" % h, "y", ["q%d" % (3 + h)], "sto", T.oc[:, 4 * lo:4 * hi], q[:, lo:hi].bitcast(dt.uint8))
+        dma("y%d" % h, "s", ["ya%d" % h], "sto", T.y[:, lo:hi], T.ya[:, lo:hi])
     for i in range(4):
-        dma("y", [h_q], "sto", T.osc[4 * i:4 * i + 4, :], p[32 * i:32 * i + 4, :])
-    dma("y", [h0], "sto", T.y[:, 0:HALF], T.ya[:, 0:HALF])
-    dma("s", [h1], "sto", T.y[:, HALF:C], T.ya[:, HALF:C])
-    wait("g", list(done.items()))
+        dma("osc%d" % i, "ys"[i // 2], ["q3", "q4"], "sto", T.osc[4 * i:4 * i + 4, :], p[32 * i:32 * i + 4, :])
+    return calls
+
+
+def in_order(calls):
+    order = {}
+    lines = [line.split() for line in ORDER.strip().split("\n")]
+    for part, r in (("A", 0), ("B", 0), ("B", 1), ("C", 0)):
+        for line in lines:
+            if line[0] == part:
+                names = [w.rstrip("+") + str(r + w.count("+")) for w in line[2:]] if part == "B" else line[2:]
+                order.setdefault(line[1], []).extend(w for w in names if w in calls and calls[w][0] == line[1])
+    return order
+
+
+def rank_program(g, core, T, topo):
+    if T.rank_of(core) is None:
+        return
+    calls = plan(g, core, T, topo)
+    order = in_order(calls)
+    Q = {"v": g.vector, "s": g.scalar, "t": g.tensor, "g": g, "y": g.sync}
+    total, mark = {}, {}
+    for q in order:
+        for name in order[q]:
+            s, n = calls[name][2]
+            total[s] = total.get(s, 0) + n
+            mark[name] = (s, total[s])
+    assert len(mark) == len(calls)
+
+    def wait(q, seen, marks):
+        need = {}
+        for s, n in marks:
+            need[s] = max(need.get(s, 0), n)
+        for s, n in need.items():
+            if seen.get(s, 0) < n:
+                Q[q].wait_ge(T.sem[s], n)
+                seen[s] = n
+
+    for q in order:
+        seen = {}
+        for name in order[q]:
+            wait(q, seen, [mark[d] if isinstance(d, str) else d[:2] for d in calls[name][1]])
+            calls[name][3]()
+        if q == "g":
+            wait(q, seen, total.items())

from concourse.mybir import dt, AluOpType, ActivationFunctionType

C, K = 352, 22
HALF = 176
BIG = 2.0 ** 30
STEP = [1, 2, 4]
NJ = 8
DUP = ["vvvvvvv", "vvvvvvv", "vvvvvvv"]
HOME = ["vvvs", "vvvs", "vvssvvss"]
TWIN = ["yyyy", "vyvy", "vvvv"]
MEAN = ["sssh", "sssh", "sssh"]
SIGN = ["v", "s", "s"]
KEEP = ["ssss", "ssss", "ssss"]
FAR = ["ssss", "ssss", "svsv"]
OUT = ["ssss", "ssss", "svvs"]
EARLY = [False, False, True]
SPJ = [False, False, False]
SPL = [False, False, False]
SPT = [True, True, True]
PARTS = [(0, 192), (192, C)]

ORDER = """
A g ul dd pc idn so0 si0 so1
A y lod lu lx lv fe00 lp lw fe30 fe20 fe10
A t ms0 mf00 mf30 mf20 mf10
A v ones e uo o0 e0 e2 dm ma mb uq e3 mk16 row0 sc e1 eq n0 i0 uc q0
A v s00 t00 l00 sign0 s10 t10 d10 of l10 s20 t20 d20 pa0 l20 s30 t30 d30 l30 s40 t40 d40 pb0 l40 s50 t50 d50 l50
A v s60 t60 d60 l60 s70 d70 t70 l70 l80 s80 L80 t80 S80 vq T80 pc0 os0 OS0 om0 oa0 o1
A s mk32 up mk64 mk128 mk256 mk j00 j10 f00 j20 j30 f30 j40 j50 f20 j60 f10 j70 place0 flag0 FLAG0 fcol0
B g si+ sc sp xc+ xp+ sn+ so++
B y fe1+ fe3+
B t mr1 mr0 mr3 mr2 mf1+ ms+ mf2+ mf0+ md3+ md1+ md0+ md2+ mf3+
B v a0 is im ia i+ a1 a2 a3 w3 zq pa+
B v s0+ t0+ l0+ pb+ s1+ t1+ d1+ l1+ s2+ t2+ d2+ l2+ s3+ t3+ d3+ l3+ s4+ d4+ t4+
B v x1 l4+ s5+ x0 d5+ t5+ x2 l5+ s6+ x3 t6+ d6+ q+ l6+
B v s7+ d7+ t7+ l7+ l8+ s8+ L8+ t8+ S8+ pc+ T8+ fe2+ os+ fe0+ OS+ om+ oa+ o++
B s z0 row+ z1 z2 z3 j0+ j1+ j2+ j3+ j4+
B s r1 r0 j5+ r3 r2 h3 j6+ j7+ f1+ sign+ place+ f2+ f0+ flag+ FLAG+ f3+ fcol+
C y fo oc0 oc1 osc1 osc0
C t mr32 mr22 mr12 mr02 my0 my1
C v is2 g32 im2 g12 ia2 ge32 ge02 ge12 ge22 a02 a22 a12 a32 w32 zq2 i3 r22 r12 x32 x12 x22 x02 x72 q3 x42 x62 x52 q4 ya1
C s k02 g02 g22 fr k12 z02 z22 z12 z32 r32 h32 h22 r02 h72 h62 ya0 y0 osc3 osc2 y1
"""

SCRATCH = {
    "odl": ("sbuf", [128, K], "int32"), "pc": ("sbuf", [128, C], "bfloat16"),
    "dd": ("sbuf", [128, 16], "int32"), "dm": ("sbuf", [128, 16], "int32"),
    "ma": ("sbuf", [128, 16], "float32"), "mb": ("sbuf", [128, 16], "float32"),
    "mk": ("sbuf", [128, C], "bfloat16"), "sc": ("sbuf", [128, 1], "float32"),
    "ones": ("sbuf", [128, 128], "bfloat16"), "idn": ("sbuf", [128, 128], "bfloat16"),
    "et": ("sbuf", [128, 2048], "bfloat16"),
    "eq": ("sbuf", [128, 512], "float8_e4m3fn_x4"), "es": ("sbuf", [128, 512], "uint8"),
    "ut": ("sbuf", [128, 512], "bfloat16"), "vt": ("sbuf", [128, 512], "bfloat16"),
    "uq": ("sbuf", [128, 128], "float8_e4m3fn_x4"), "us": ("sbuf", [128, 128], "uint8"),
    "u2q": ("sbuf", [128, 128], "float8_e4m3fn_x4"), "u2s": ("sbuf", [128, 128], "uint8"),
    "ul": ("sbuf", [128, 8], "int32"), "uo": ("sbuf", [128, 8], "uint16"),
    "vq": ("sbuf", [128, 128], "float8_e4m3fn_x4"), "vs": ("sbuf", [128, 128], "uint8"),
    "wq": ("sbuf", [128, 512], "float8_e4m3fn_x4"), "wp": ("sbuf", [128, 512], "uint8"),
    "ps": ("psum", [128, 4096], "float32"),
    "ya": ("sbuf", [128, C], "float32"), "fr": ("sbuf", [128, C], "float32"), "s0": ("sbuf", [128, C], "bfloat16"),
}
for _r in range(4):
    SCRATCH["x%d" % _r] = ("sbuf", [128, 4 * C], "bfloat16")
    SCRATCH["xq%d" % _r] = ("sbuf", [128, C], "float8_e4m3fn_x4")
    SCRATCH["xs%d" % _r] = ("sbuf", [128, C], "uint8")
    SCRATCH["o%d" % _r] = ("sbuf", [128, 2 * K], "uint16")
    SCRATCH["of%d" % _r] = ("sbuf", [128, 2 * K], "float32")
for _r in range(3):
    _d = "bfloat16"
    SCRATCH["inv%d" % _r] = ("sbuf", [128, C], "bfloat16")
    SCRATCH["oin%d" % _r] = ("sbuf", [128, 2 * K], "uint16")
    SCRATCH["f%d" % _r] = ("sbuf", [128, 4 * C], "bfloat16")
    SCRATCH["fe%d" % _r] = ("sbuf", [128, 4 * C], "bfloat16")
    SCRATCH["a%d" % _r] = ("sbuf", [128, 4 * C], "float32")
    SCRATCH["z%d" % _r] = ("sbuf", [128, 4 * C], "bfloat16")
    SCRATCH["zq%d" % _r] = ("sbuf", [128, C], "float8_e4m3fn_x4")
    SCRATCH["zs%d" % _r] = ("sbuf", [128, C], "uint8")
    SCRATCH["zi%d" % _r] = ("sbuf", [128, C], "float8_e4m3fn_x4")
    SCRATCH["zp%d" % _r] = ("sbuf", [128, C], "uint8")
    SCRATCH["rb%d" % _r] = ("sbuf", [128, 4 * C], "float32")
    SCRATCH["hs%d" % _r] = ("sbuf", [128, 4 * C], "float32")
    SCRATCH["jr%d" % _r] = ("sbuf", [128, NJ * C], "bfloat16")
    SCRATCH["lr%d" % _r] = ("sbuf", [128, 9 * C], _d)
    SCRATCH["le%d" % _r] = ("sbuf", [128, NJ * C], _d)
    SCRATCH["sr%d" % _r] = ("sbuf", [128, 11 * C], "bfloat16")
    SCRATCH["tb%d" % _r] = ("sbuf", [128, 9 * K], "uint16")
    SCRATCH["sg%d" % _r] = ("sbuf", [128, 4 * C], "bfloat16")
    SCRATCH["sm%d" % _r] = ("sbuf", [128, 8 * K], "float32")
    if EARLY[_r]:
        SCRATCH["fd%d" % _r] = ("sbuf", [128, 4 * C], "bfloat16")
        SCRATCH["oz%d" % _r] = ("sbuf", [128, K], "uint16")
SEMAPHORES = (["sv", "ss", "st", "sg", "loc", "sto"] + ["l" + n for n in ("od", "x", "u", "v", "w", "p")]
              + [n + str(r) for n in ("ro", "ri", "rz") for r in range(3)]
              + ["fe%d%d" % (b, r) for b in range(4) for r in range(3) if TWIN[r][b] == "y"]
              + ["rn%d" % r for r in range(3) if EARLY[r]])
OWN = {"v": "sv", "s": "ss", "t": "st", "g": "sg"}


def plan(g, core, T, topo):
    rank = T.rank_of(core)
    A, F = AluOpType, ActivationFunctionType
    V, S, PE, Y = g.vector, g.scalar, g.tensor, g.sync
    calls = {}
    partner = [T.cores[rank ^ s] for s in STEP]

    def do(name, q, after, call, *args, **kw):
        calls[name] = (q, after, (OWN[q], 1), lambda: call(*args, **kw).then_inc(T.sem[OWN[q]], 1))

    def dma(name, q, after, s, out, in_):
        calls[name] = (q, after, (s, 16), lambda: {"y": Y, "s": S}[q].dma_start(out, in_).then_inc(T.sem[s], 16))

    def send(name, after, dst, s, out, in_):
        rid, pid = topo.addr(dst)[:2]
        calls[name] = ("g", after, ("loc", len(topo.engines(core, dst))),
                       lambda: g.remote_dma(out, in_, T.sem[s], T.sem["loc"], pid, rid, topo.mask(core, dst)))

    def landed(s, r, *names):
        return (s + str(r), len(names) * len(topo.engines(partner[r], core)), names)

    def blk(t, b, n=C):
        return t[:, b * n:(b + 1) * n]

    def bank(k, lo=0, hi=C):
        return T.ps[:, 512 * k + lo:512 * k + hi]

    def mm(name, after, k, a, ap, ca, b, bp, lo=0, hi=C):
        do(name, "t", after, PE.matmul_mx, bank(k, 0, hi - lo), a[:, ca:ca + 128], ap[:, ca:ca + 128],
           b[:, lo:hi], bp[:, lo:hi], True, True)

    def scan(name, after, out, k, rows, i, lo=0, hi=C):
        do(name, "v", after + ["mk"], V.tensor_tensor_scan, out[:, k * C + lo:k * C + hi], T.mk[:, lo:hi],
           rows[:, i * C + lo:i * C + hi], 0.0, A.mult, A.add)

    def ends(t, k, lo=0, hi=C):
        return t[:, k * C + lo + 15:k * C + hi:16]

    def table(name, after, out, t, k, lo=0, hi=C):
        do(name, "v", after + ["sc"], V.tensor_scalar, out, ends(t, k, lo, hi), T.sc[:], HALF + 0.25, A.mult, A.add)

    def again(name, q, after, out, in_):
        if q == "s":
            do(name, q, after, S.activation, out, in_, F.Copy)
        elif q == "v":
            do(name, q, after, V.tensor_copy, out, in_)
        else:
            do(name, q, after, g.affine_select, out, in_, [[0, C]], A.is_ge, 0.0, 0, 0)

    dma("lod", "y", [], "lod", T.odl[:], T.od[:, :])
    dma("lx", "y", [], "lx", T.x0[:], T.x[:, :])
    dma("lu", "y", [], "lu", T.ut[:], T.u[:, :])
    dma("lw", "y", [], "lw", T.wq[:].bitcast(dt.uint8), T.wc[:, :])
    dma("lp", "y", [], "lp", T.wp[:], T.ws[:, :])
    dma("lv", "y", [], "lv", T.vt[:], T.v[:, :])
    do("dd", "g", [], g.iota, T.dd[:], [[1, 16]], 128, -1)
    do("ul", "g", [], g.iota, T.ul[:], [[16, 8]], 0, 0)
    do("ones", "v", [], V.memset, T.ones[:], 1.0)
    do("idn", "g", ["ones"], g.affine_select, T.idn[:], T.ones[:], [[-1, 128]], A.is_equal, 0.0, 0, 1)
    do("pc", "g", [], g.iota, T.pc[:], [[1, C]], -HALF, 0, allow_small_or_imprecise_dtypes=True)
    do("e", "v", [], V.memset, T.et[:], 0.0)
    do("dm", "v", ["dd"], V.tensor_scalar, T.dm[:], T.dd[:], 15, None, A.bitwise_and)
    do("sc", "v", ["dm"], V.tensor_scalar, T.sc[:], T.dm[:, 0:1], 1, 1.0 / BIG, A.is_equal, A.max)
    do("ma", "v", ["dm"], V.tensor_scalar, T.ma[:], T.dm[:], 1, BIG, A.is_equal, A.mult)
    do("mb", "v", ["dm"], V.tensor_scalar, T.mb[:], T.dm[:], 2, None, A.is_ge)
    do("mk16", "v", ["ma", "mb"], V.tensor_tensor, T.mk[:, 0:16], T.ma[:], T.mb[:], A.add)
    for n in (16, 32, 64, 128, 256):
        m = min(n, C - n)
        do("mk%d" % (n + m) if n + m < C else "mk", "s", ["mk%d" % n], S.activation, T.mk[:, n:n + m], T.mk[:, 0:m], F.Copy)
    for b in range(4):
        do("e%d" % b, "v", ["e", "idn"], V.tensor_copy, T.et[:, 512 * b + b:512 * (b + 1):4], T.idn[:])
    do("eq", "v", ["e0", "e1", "e2", "e3"], V.quantize_mx, T.eq[:], T.es[:], T.et[:])
    do("uo", "v", ["ul"], V.tensor_copy, T.uo[:], T.ul[:])
    do("uq", "v", ["lu"], V.quantize_mx, T.uq[:], T.us[:], T.ut[:])
    do("uc", "v", ["uq", "uo"], V.tensor_copy, T.u2q[:].bitcast(dt.uint32), T.uq[:].bitcast(dt.uint32).indirect(T.uo[:]))
    do("up", "s", ["uq", "uo"], S.activation, T.u2s[:], T.us[:].indirect(T.uo[:]), F.Copy)
    do("vq", "v", ["lv"], V.quantize_mx, T.vq[:], T.vs[:], T.vt[:])
    do("o0", "v", ["lod"], V.tensor_copy, blk(T.o0, 0, K), T.odl[:])
    do("row0", "v", ["o0", "pc"], V.tensor_copy, T.inv0[:].indirect(blk(T.o0, 0, K)), T.pc[:])
    scan("n0", ["row0"], T.s0, 0, T.inv0, 0)
    table("i0", ["n0"], blk(T.o0, 1, K), T.s0, 0)
    do("of", "v", ["o0", "i0"], V.tensor_scalar, T.of0[:], T.o0[:], 0.25, None, A.add)
    do("q0", "v", ["lx"], V.quantize_mx, T.xq0[:], T.xs0[:], T.x0[:])

    for r in range(3):
        def n(s, r=r):
            return s + str(r)
        o, on, of, ofn = T[n("o")], T[n("o", r + 1)], T[n("of")], T[n("of", r + 1)]
        oin, inv, tb, jr, lr, le, sr, sg, sm = (T[n(s)] for s in ("oin", "inv", "tb", "jr", "lr", "le", "sr", "sg", "sm"))
        f, fe, a, z, rb, hs, xn = T[n("f")], T[n("fe")], T[n("a")], T[n("z")], T[n("rb")], T[n("hs")], T[n("x", r + 1)]
        xq, xs, zq, zs, zi, zp = (T[n(s)] for s in ("xq", "xs", "zq", "zs", "zi", "zp"))
        send(n("so"), [n("o")], partner[r], n("ro"), blk(oin, 0, K), blk(o, 0, K))
        send(n("si"), [n("i")], partner[r], n("ri"), blk(oin, 1, K), blk(o, 1, K))
        there = landed("ro", r, n("so"))
        sent = ("xc", "xp") if EARLY[r] else ("sc", "sp")
        codes = landed("rz", r, n(sent[0]), n(sent[1]))
        parts = PARTS if r == 2 else [(0, C)]
        mm(n("ms"), [n("q"), "uc", "up"], 0, T.u2q, T.u2s, 0, xq, xs)
        if SIGN[r] == "s":
            do(n("sign"), "s", [n("ms")], S.activation, blk(sg, 0), bank(0), F.Sign)
        else:
            do(n("sign"), "v", [n("ms")], V.tensor_scalar, blk(sg, 0), bank(0), 0.0, None, A.is_gt)
        do(n("place"), "s", [n("sign"), n("o")], S.activation, blk(sg, 1), blk(sg, 0).indirect(blk(o, 0, K)), F.Relu)
        kept, twin = [], []
        for b in range(4):
            mm(n("mf%d" % b), [n("q"), "eq"], 1 + b, T.eq, T.es, 128 * b, xq, xs)
            kept.append(n("mf%d" % b))
            if not EARLY[r] or "v" in HOME[r][b::4]:
                kept[b] = n(("k%d" if EARLY[r] else "f%d") % b)
                again(kept[b], KEEP[r][b], [n("mf%d" % b)], blk(f, b), bank(1 + b))
            if EARLY[r]:
                k = (5 + b) % 8
                mm(n("md%d" % b), [codes, "eq", n("sign")], k, T.eq, T.es, 128 * b, zi, zp)
                again(n("g%d" % b), FAR[r][b], [n("md%d" % b)], blk(T[n("fd")], b), bank(k))
            first, row = (n("g%d" % b), blk(T[n("fd")], b)) if EARLY[r] else (n("f%d" % b), blk(f, b))
            twin.append(n(("ge%d" if EARLY[r] else "fe%d") % b))
            if TWIN[r][b] == "y":
                dma(twin[b], "y", [first], n("fe%d" % b), blk(fe, b), row)
            else:
                again(twin[b], TWIN[r][b], [first], blk(fe, b), row)
        def runs(split):
            return [(str.lower, *PARTS[0]), (str.upper, *PARTS[1])] if split else [(str.lower, 0, C)]

        def both(s, k, split, r=r):
            return [case(s) + str(k) + str(r) for case, lo, hi in runs(split)]

        def row(t, k, lo, hi):
            return t[:, k * C + lo:k * C + hi]

        def tab(t, k, lo, hi):
            return t[:, k * K + lo // 16:k * K + hi // 16]

        def tables(k, split, h):
            return both("t", k, sj)[h:h + 1] if split and sj else both("t", k, sj)

        sj, sl, st = SPJ[r], SPL[r], SPT[r]
        for k in range(NJ):
            for h, (case, lo, hi) in enumerate(runs(sj)):
                if k:
                    do(n(case("j%d" % k)), "s", both("j", k - 1, sj) + tables(k - 1, sj, h), S.activation,
                       row(jr, k, lo, hi), blk(jr, k - 1).indirect(tab(tb, k - 1, lo, hi)), F.Copy)
                else:
                    do(n(case("j0")), "s", [there, n("row")], S.activation, row(jr, 0, lo, hi), inv[:].indirect(tab(oin, 0, lo, hi)), F.Copy)
                scan(n(case("s%d" % k)), [n(case("j%d" % k))], sr, k, jr, k, lo, hi)
                table(n(case("t%d" % k)), [n(case("s%d" % k))], tab(tb, k, lo, hi), sr, k, lo, hi)
            for h, (case, lo, hi) in enumerate(runs(sl)):
                if k:
                    again(n(case("d%d" % k)), DUP[r][k - 1], [n(case("l%d" % (k - 1)))], row(le, k, lo, hi), row(lr, k - 1, lo, hi))
                    do(n(case("l%d" % k)), "v", both("l", k - 1, sl) + tables(k, sl, h) + [n(case("d%d" % k))], V.tensor_tensor,
                       row(lr, k, lo, hi), blk(lr, k - 1).indirect(tab(tb, k, lo, hi)), row(le, k, lo, hi), A.min)
                else:
                    do(n(case("l0")), "v", [there, n("row"), "pc"], V.tensor_tensor,
                       row(lr, 0, lo, hi), inv[:].indirect(tab(oin, 0, lo, hi)), T.pc[:, lo:hi], A.min)
        for case, lo, hi in runs(st):
            do(n(case("l8")), "v", both("l", 7, sl), V.tensor_tensor,
               row(lr, 8, lo, hi), blk(lr, 7).indirect(tab(tb, 7, lo, hi)), row(lr, 6, lo, hi), A.min)
            scan(n(case("s8")), [n(case("l8"))], sr, 8, lr, 8, lo, hi)
            table(n(case("t8")), [n(case("s8"))], tab(tb, 8, lo, hi), sr, 8, lo, hi)
            do(n(case("flag")), "s", [n("place"), n(case("t8"))], S.activation,
               row(sg, 2, lo, hi), blk(sg, 1).indirect(tab(tb, 8, lo, hi)), F.Copy)
            scan(n(case("os")), [n(case("flag"))], sr, 9, sg, 2, lo, hi)
        do(n("pa"), "v", [there, landed("ri", r, n("si"))], V.tensor_scalar, blk(sm, 0, 2 * K), oin[:], 0.25, None, A.add)
        do(n("pb"), "v", [n("pa")] + (["of"] if r == 0 else [n("oa", r - 1), n("ia", r - 1)]), V.tensor_tensor,
           blk(sm, 1, 2 * K), blk(sm, 0, 2 * K), of[:], A.subtract)
        do(n("pc"), "v", [n("pb"), "sc"], V.tensor_scalar, blk(sm, 2, 2 * K), blk(sm, 1, 2 * K), T.sc[:], None, A.mult)
        do(n("fcol"), "s", both("flag", "", st) + [n("i")], S.activation, blk(sg, 3), blk(sg, 2).indirect(blk(o, 1, K)), F.Copy)
        scan(n("is"), [n("fcol")], sr, 10, sg, 3)
        for h, s in enumerate("oi"):
            do(n(s + "m"), "v", both(s + "s", "", st and h == 0) + [n("pc")], V.tensor_tensor,
               blk(sm, 6 + h, K), ends(sr, 9 + h), blk(sm, 4 + h, K), A.mult)
            do(n(s + "a"), "v", [n(s + "m")], V.tensor_tensor, blk(ofn, h, K), blk(sm, 6 + h, K), blk(of, h, K), A.add)
            do(n(s, r + 1), "v", [n(s + "a")], V.tensor_copy, blk(on, h, K), blk(ofn, h, K))
        if r < 2:
            do(n("row", r + 1), "s", [n("i", r + 1), "pc"], S.activation, T[n("inv", r + 1)][:], T.pc[:].indirect(blk(on, 1, K)), F.Copy)
        if EARLY[r]:
            send(n("sn"), [n("o", r + 1)], partner[r], n("rn"), T[n("oz")][:], blk(on, 0, K))
            by, known, d, out, made = T[n("oz")], landed("rn", r, n("sn")), T[n("fd")], (xq, xs), n("q")
        else:
            by, known, d, out, made = on, n("o", r + 1), f, (zq, zs), n("zq")
        means = []
        for b in range(4):
            do(n("a%d" % b), "v", [known, twin[b]], V.tensor_tensor, blk(a, b), blk(d, b).indirect(by[:, 0:K]), blk(fe, b), A.add)
            lo = PARTS[1][0] if MEAN[r][b] == "h" else C
            do(n("z%d" % b), "s", [n("a%d" % b), known], S.activation, z[:, b:4 * lo:4], blk(a, b).indirect(by[:, 0:lo // 16]), F.Copy, scale=0.5)
            means.append(n("z%d" % b))
            if lo < C:
                do(n("w%d" % b), "v", [n("a%d" % b)], V.tensor_scalar, z[:, 4 * lo + b:4 * C:4], blk(a, b).indirect(by[:, lo // 16:K]), 0.5, None, A.mult)
                means.append(n("w%d" % b))
        do(n("zq"), "v", means, V.quantize_mx, zq[:], zs[:], z[:])
        send(n(sent[0]), [made], partner[r], n("rz"), zi[:].bitcast(dt.uint8), out[0][:].bitcast(dt.uint8))
        send(n(sent[1]), [made], partner[r], n("rz"), zp[:], out[1][:])
        for b in range(4):
            k = (5 + b) % 8
            if EARLY[r]:
                mm(n("mr%d" % b), [n("zq"), "lw", "lp"], k, T.wq, T.wp, 128 * b, zq, zs)
            else:
                mm(n("mr%d" % b), [codes, "lw", "lp", n("sign")], k, T.wq, T.wp, 128 * b, zi, zp)
            if OUT[r][b] == "s":
                do(n("r%d" % b), "s", [n("mr%d" % b)], S.activation, blk(rb, b), bank(k), F.Copy, scale=0.03125)
            else:
                do(n("r%d" % b), "v", [n("mr%d" % b)], V.tensor_scalar, blk(rb, b), bank(k), 0.03125, None, A.mult)
            for h, (lo, hi) in enumerate(parts):
                at_home, i = blk(rb, b).indirect(on[:, K + lo // 16:K + hi // 16]), b + 4 * h
                to = xn[:, 4 * lo + b:4 * hi:4]
                if HOME[r][i] == "v":
                    do(n("x%d" % i), "v", [n("r%d" % b), n("i", r + 1), kept[b]], V.tensor_tensor, to, at_home, f[:, b * C + lo:b * C + hi], A.add)
                else:
                    do(n("h%d" % i), "s", [n("r%d" % b), n("i", r + 1)], S.activation, hs[:, b * C + lo:b * C + hi], at_home, F.Copy)
                    do(n("x%d" % i), "v", [n("h%d" % i), kept[b]], V.tensor_tensor, to, bank(1 + b, lo, hi), hs[:, b * C + lo:b * C + hi], A.add)
        for h, (lo, hi) in enumerate(parts):
            do(n("q", r + 1 + h), "v", [n("x%d" % (b + 4 * h)) for b in range(4)], V.quantize_mx,
               T[n("xq", r + 1)][:, lo:hi], T[n("xs", r + 1)][:, lo:hi], xn[:, 4 * lo:4 * hi])
    do("fr", "s", ["o3", "pc"], S.activation, T.fr[:], T.pc[:].indirect(blk(T.o3, 0, K)), F.Identity, bias=float(HALF))
    dma("fo", "y", ["fr"], "sto", T.fo[:, :], T.fr[0:128:16, :])
    q, p = T.xq3, T.xs3
    for h, (lo, hi) in enumerate(PARTS):
        mm("my%d" % h, ["q%d" % (3 + h), "vq", "r02", "r12"], 5 + h, T.vq, T.vs, 0, q, p, lo, hi)
        again("ya%d" % h, "sv"[h], ["my%d" % h], T.ya[:, lo:hi], bank(5 + h, 0, hi - lo))
        dma("oc%d" % h, "y", ["q%d" % (3 + h)], "sto", T.oc[:, 4 * lo:4 * hi], q[:, lo:hi].bitcast(dt.uint8))
        dma("y%d" % h, "s", ["ya%d" % h], "sto", T.y[:, lo:hi], T.ya[:, lo:hi])
    for i in range(4):
        dma("osc%d" % i, "ys"[i // 2], ["q3", "q4"], "sto", T.osc[4 * i:4 * i + 4, :], p[32 * i:32 * i + 4, :])
    return calls


def in_order(calls):
    order = {}
    lines = [line.split() for line in ORDER.strip().split("\n")]
    for part, r in (("A", 0), ("B", 0), ("B", 1), ("C", 0)):
        for line in lines:
            if line[0] == part:
                names = [w.rstrip("+") + str(r + w.count("+")) for w in line[2:]] if part == "B" else line[2:]
                order.setdefault(line[1], []).extend(w for w in names if w in calls and calls[w][0] == line[1])
    return order


def rank_program(g, core, T, topo):
    if T.rank_of(core) is None:
        return
    calls = plan(g, core, T, topo)
    order = in_order(calls)
    Q = {"v": g.vector, "s": g.scalar, "t": g.tensor, "g": g, "y": g.sync}
    total, mark = {}, {}
    for q in order:
        for name in order[q]:
            s, n = calls[name][2]
            total[s] = total.get(s, 0) + n
            mark[name] = (s, total[s])
    assert len(mark) == len(calls)

    def wait(q, seen, marks):
        need = {}
        for s, n in marks:
            need[s] = max(need.get(s, 0), n)
        for s, n in need.items():
            if seen.get(s, 0) < n:
                Q[q].wait_ge(T.sem[s], n)
                seen[s] = n

    for q in order:
        seen = {}
        for name in order[q]:
            wait(q, seen, [mark[d] if isinstance(d, str) else d[:2] for d in calls[name][1]])
            calls[name][3]()
        if q == "g":
            wait(q, seen, total.items())
